import numpy as np
import ml_dtypes


def mxq(x, axis, fmt="e4m3"):
    dtype, down = {"e4m3": (ml_dtypes.float8_e4m3fn, 7), "e5m2": (ml_dtypes.float8_e5m2, 14)}[fmt]
    v = np.moveaxis(np.asarray(x, np.float32).astype(ml_dtypes.bfloat16).astype(np.float64), axis, -1)
    blocks = v.reshape(v.shape[:-1] + (-1, 32))
    amax = np.abs(blocks).max(-1, keepdims=True)
    byte = np.maximum(np.where(amax > 0, np.frexp(amax)[1] - 1 + 127, 0) - down, 1)
    scale = np.exp2(byte - 127.0)
    codes = (blocks / scale).astype(np.float32).astype(dtype).astype(np.float64)
    return np.moveaxis((codes * scale).reshape(v.shape), -1, axis)


WIDE = False


def mx_kscale(k):
    if not WIDE:
        return np.ones(k)
    levels = np.array([10, -10, 5, -5, 0])
    if k % 512:
        return np.exp2(np.random.permutation(np.resize(levels, k // 32))).repeat(32)
    a = np.empty((k // 512, 16))
    for p in range(k // 512):
        a[p, :8] = np.random.permutation(np.resize(levels, 8))
        for g in range(8):
            far = levels[np.abs(levels - a[p, g]) >= 10]
            a[p, g + 8] = far[np.random.randint(len(far))]
    return np.exp2(a.ravel()).repeat(32)


BF16 = ml_dtypes.bfloat16


def bf(x):
    return np.asarray(x, np.float32).astype(BF16)


def f64(x):
    return np.asarray(x).astype(np.float64)

def planes(Y):
    n, m = Y.shape
    b = f64(bf(Y)).reshape(n // 32, 32, m)
    amax = np.abs(b).max(1)
    byte = np.clip(np.where(amax > 0, np.frexp(amax)[1] - 1 + 127 - 7, 1), 1, 254)
    codes = (b * np.exp2(127.0 - byte)[:, None, :]).reshape(n, m).astype(np.float32).astype(ml_dtypes.float8_e4m3fn).view(np.uint8)
    words = codes.reshape(n // 512, 128, 4, m).transpose(0, 1, 3, 2)
    return np.ascontiguousarray(words), np.ascontiguousarray(byte.astype(np.uint8).reshape(n // 512, 16, m))


A, K, P, D = 1536, 2048, 512, 1024

def setup_inputs():
    s = mx_kscale(K)
    u = mx_kscale(A)
    t = mx_kscale(A)
    signals = np.random.randn(A, K) * s[None, :]
    alpha = np.random.randn(K, P) / np.sqrt(K) / s[:, None]
    limit = 0.25 * np.exp(0.3 * np.random.randn(A)) * t
    risk = 0.4 * np.random.randn(A, A) / np.sqrt(A) * u[None, :] / t[:, None]
    directions = np.random.randn(A, D) / u[:, None]
    views = 0.5 * np.random.randn(P, D)
    aversion = 0.5 * np.exp(0.8 * np.random.randn(D))
    return {"signals": bf(signals), "alpha": bf(alpha), "limit": bf(limit),
            "risk": bf(risk), "directions": bf(directions),
            "views": bf(views), "aversion": bf(aversion)}

def reference(signals, alpha, limit, risk, directions, views, aversion):
    sq = mxq(f64(signals), 1, "e4m3")
    wq = mxq(f64(alpha), 0, "e4m3")
    positions = np.tanh(sq @ wq) * f64(limit)[:, None]
    cq = mxq(f64(risk), 1, "e4m3")
    rq = mxq(f64(directions), 0, "e4m3")
    drag = -(cq @ rq)
    pq = mxq(positions, 0, "e4m3")
    dq = mxq(drag, 0, "e4m3")
    y = ((pq.T @ dq) + f64(views)) * f64(aversion)[None, :]
    Y = y.T
    words, scales = planes(Y)
    return y, words, scales

@@ -1,0 +1,351 @@
+from collections import defaultdict
+from contextlib import ExitStack
+
+import concourse.mybir as mybir
+from concourse.masks import make_identity
+
+A, K, B, D = 1536, 2048, 512, 1024
+FLOPS = 2 * A * K * B + 2 * A * A * D + 2 * A * B * D
+
+F32 = mybir.dt.float32
+BF16 = mybir.dt.bfloat16
+U32 = mybir.dt.uint32
+I32 = mybir.dt.int32
+U8 = mybir.dt.uint8
+FP8X4 = mybir.dt.float8_e4m3fn_x4
+ACT = mybir.ActivationFunctionType
+ALU = mybir.AluOpType
+
+P = 128
+PACK = 4
+PASS = P * PACK
+GROUPS = A // PASS
+CHUNKS = B // P
+HALVES = D // PASS
+RAW_BUFS = 10
+SORT_LEAD = 5
+QUANT_LAG = 2
+SORT_FROM = 2
+Y_ADD, Y_MUL, Y_CAST = 1, 2, 3
+P_MUL, P_Q = 1, 2
+T_LAG = 2
+PLAN = 1
+ORD = 0
+TY_LAG=2
+ENG_A = "vector"
+
+
+def tile_book_risk_drag_h3_kernel(
+    tc, signals, alpha, limit, risk, directions, views, aversion, out_0, out_1, out_2
+):
+    nc = tc.nc
+    with ExitStack() as ctx:
+        keep = ctx.enter_context(tc.tile_pool(name="keep", bufs=1))
+        raw_pool = ctx.enter_context(tc.tile_pool(name="raw", bufs=RAW_BUFS))
+        stage = ctx.enter_context(tc.tile_pool(name="stage", bufs=3))
+        psum = ctx.enter_context(tc.psum_pool(name="psum", bufs=8))
+        ctx.enter_context(tc.manual_schedule())
+
+        ident = keep.tile([P, P], F32, name="ident")
+        make_identity(nc, ident[:])
+
+        def mx_tiles(name, width, pool=keep, tag=None, bufs=None):
+            codes = pool.tile([P, width], U32, name=name + "_codes", tag=(tag or name) + "_codes", bufs=bufs, align_bytes=64)
+            scales = pool.tile([P, width], U8, name=name + "_scales", tag=(tag or name) + "_scales", bufs=bufs, align_bytes=64)
+            return codes, scales
+
+        def window(mx, i, width):
+            cols = slice(i * width, (i + 1) * width)
+            return mx[0][:, cols], mx[1][:, cols]
+
+        def quantize(mx, src):
+            nc.vector.quantize_mx(out=mx[0].bitcast(FP8X4), scales=mx[1], in_=src)
+
+        def matmul(out, stationary, moving, start, stop):
+            nc.tensor.matmul_mx(
+                out=out, lhsT=stationary[0].bitcast(FP8X4), lhsT_scale=stationary[1],
+                rhs=moving[0].bitcast(FP8X4), rhs_scale=moving[1], start=start, stop=stop,
+            )
+
+        def bank_tile():
+            return psum.tile([P, PASS], F32, name="bank")
+
+        row_major = {"risk": risk, "signals": signals}
+        passes = {"risk": A // PASS, "signals": K // PASS}
+        order = []
+        for t in range(PACK):
+            order.append(("risk", 0, t))
+            if t < GROUPS:
+                order.append(("directions", 0, t))
+        order.extend(("risk", g, t) for g in (1, 2) for t in range(PACK))
+        order.extend(("directions", 1, a) for a in range(GROUPS))
+        order.extend(("signals", 0, t) for t in range(PACK))
+        order.extend(("alpha", 0, a) for a in range(passes["signals"]))
+        order.extend(("signals", g, t) for g in (1, 2) for t in range(PACK))
+        raw = {}
+        consumed = set()
+        small = {}
+
+        def load(key):
+            name, i, j = key
+            if name in row_major:
+                src = row_major[name][i * PASS:(i + 1) * PASS, :].rearrange("(m t) k -> m t k", t=PACK)[:, j, :]
+                tile = raw_pool.tile([P, passes[name] * PASS], BF16, name="raw")
+                nc.sync.dma_start(out=tile[:], in_=src)
+            else:
+                matrix = directions if name == "directions" else alpha
+                src = matrix[j * PASS:(j + 1) * PASS, i * PASS:(i + 1) * PASS].rearrange("(p t) n -> p t n", t=PACK)
+                tile = raw_pool.tile([P, PACK, PASS], BF16, name="raw")
+                nc.sync.dma_start(out=tile[:], in_=src)
+            raw[key] = tile
+
+        def load_small():
+            small["limit"] = keep.tile([P, GROUPS, PACK], BF16, name="limit_sb")
+            nc.sync.dma_start(out=small["limit"][:], in_=limit.rearrange("(g p t) -> p g t", p=P, t=PACK))
+
+        def load_last():
+            small["views"] = keep.tile([P, CHUNKS, D], BF16, name="views_sb")
+            nc.sync.dma_start(out=small["views"][:], in_=views.rearrange("(c p) d -> p c d", p=P))
+            small["aversion"] = keep.tile([P, D], BF16, name="aversion_sb")
+            nc.sync.dma_start(out=small["aversion"][:], in_=aversion.partition_broadcast(P))
+
+        def issue_loads():
+            while len(raw) < len(order):
+                n = len(raw)
+                if n >= RAW_BUFS and any(key not in consumed for key in order[: n - RAW_BUFS + 1]):
+                    return
+                load(order[n])
+                if order[n] == ("alpha", 0, 0):
+                    load_small()
+                if n + 1 == len(order):
+                    load_last()
+
+        def release(key):
+            consumed.add(key)
+            issue_loads()
+
+        issue_loads()
+
+        later = defaultdict(list)
+        jobs = []
+
+        def after(tick, lag, task):
+            later[tick + lag].append((lag * ORD, task))
+
+        moving = {}
+
+        def interleave(key, tick, engine):
+            def copy():
+                grouped = stage.tile([P, PASS, PACK], BF16, name="grouped", bufs=2, align_bytes=64)
+                dst = grouped[:].rearrange("p (c i) t -> p c t i", i=4)
+                src = raw[key][:].rearrange("p t (c i) -> p c t i", i=4)
+                if engine == "vector":
+                    nc.vector.tensor_copy(out=dst, in_=src)
+                else:
+                    nc.scalar.copy(out=dst, in_=src)
+                release(key)
+                moving[key] = mx_tiles("%s_%d_%d" % key, PASS)
+                after(tick, 1, lambda: quantize(window(moving[key], 0, PASS), grouped[:].rearrange("p n t -> p (n t)")))
+            after(tick, 0, copy)
+
+        sorted_words = {}
+        stationary = {}
+
+        def sort_words(key):
+            n_pass = passes[key[0]]
+            tile = stage.tile([P, 2, n_pass, P], F32, name="sorted", bufs=4)
+            nc.vector.tensor_copy(out=tile[:], in_=raw[key][:].bitcast(F32).rearrange("p (a m u) -> p u a m", m=P, u=2))
+            release(key)
+            sorted_words[key] = tile
+
+        def transpose_job(name, g, unit):
+            n_pass = passes[name]
+            pairs = [divmod(n, n_pass) for n in (2 * unit, 2 * unit + 1)]
+            is_sorted = name == "signals" or g >= SORT_FROM
+            if is_sorted:
+                for t, a in pairs:
+                    if a == 0:
+                        after(len(jobs) - SORT_LEAD, 0, lambda t=t: sort_words((name, g, t)))
+
+            def run(tick):
+                bank = bank_tile()
+                for i, (t, a) in enumerate(pairs):
+                    for u in range(2):
+                        if is_sorted:
+                            src = sorted_words[name, g, t][:, u, a, :]
+                        else:
+                            src = raw[name, g, t][:].bitcast(F32)[:, 2 * P * a + u: 2 * P * (a + 1): 2]
+                        nc.tensor.transpose(bank[:, (2 * i + u) * P:(2 * i + u + 1) * P], src, ident[:])
+                    if not is_sorted and a == n_pass - 1:
+                        release((name, g, t))
+                turned = stage.tile([P, 2 * PASS], BF16, name="turned", bufs=4, align_bytes=64)
+                nc.scalar.copy(
+                    out=turned[:].bitcast(F32).rearrange("p (i m u) -> p i m u", i=2, u=2),
+                    in_=bank[:].rearrange("p (i u m) -> p i m u", i=2, u=2),
+                )
+                if name == "risk":
+                    mx = mx_tiles("risk_%d_%d" % (g, unit), 2 * P)
+                else:
+                    mx = mx_tiles("signals_%d_%d" % (g, unit), 2 * P, pool=stage, tag="signals", bufs=24)
+                for i, (t, a) in enumerate(pairs):
+                    stationary[name, g, t, a] = window(mx, i, P)
+                after(tick, T_LAG, lambda: quantize(window(mx, 0, 2 * P), turned[:]))
+            jobs.append(run)
+
+        drag = {(g, h): mx_tiles("drag_%d_%d" % (g, h), PASS) for g in range(GROUPS) for h in range(HALVES)}
+        positions = {}
+
+        def first_stage(bank, name, partner, g, h, c):
+            for t in range(PACK):
+                for a in range(passes[name]):
+                    matmul(bank[:, t * P:(t + 1) * P], stationary[name, g, t, a], window(moving[partner, h, a], c, P),
+                           a == 0, a == passes[name] - 1)
+
+        def drag_job(g, h, c):
+            def run(tick):
+                bank = bank_tile()
+                first_stage(bank, "risk", "directions", g, h, c)
+                rounded = stage.tile([P, P, PACK], BF16, name="drag_bf16", bufs=4, align_bytes=64)
+                nc.scalar.activation(out=rounded[:], in_=bank[:].rearrange("p (t n) -> p n t", t=PACK), func=ACT.Copy, scale=-1.0)
+                after(tick, QUANT_LAG, lambda: quantize(window(drag[g, h], c, P), rounded[:].rearrange("p n t -> p (n t)")))
+            jobs.append(run)
+
+        def positions_job(g, c):
+            def run(tick):
+                bank = bank_tile()
+                first_stage(bank, "signals", "alpha", g, 0, c)
+                squashed = stage.tile([P, P, PACK], F32, name="squashed")
+                nc.scalar.activation(out=squashed[:], in_=bank[:].rearrange("p (t n) -> p n t", t=PACK), func=ACT.Tanh)
+                rounded = stage.tile([P, P, PACK], BF16, name="positions_bf16", align_bytes=64)
+                positions[g, c] = mx_tiles("positions_%d_%d" % (g, c), P)
+                after(tick, P_MUL, lambda: nc.vector.tensor_tensor(
+                    out=rounded[:], in0=squashed[:],
+                    in1=small["limit"][:, g, :].unsqueeze(1).to_broadcast([P, P, PACK]), op=ALU.mult))
+                after(tick, P_Q, lambda: quantize(window(positions[g, c], 0, P), rounded[:].rearrange("p n t -> p (n t)")))
+            jobs.append(run)
+
+        y_words = {}
+        y_codes = [keep.tile([P, B], U32, name="y_codes_%d" % h, align_bytes=64) for h in range(HALVES)]
+        y_scales = keep.tile([P, HALVES, B], U8, name="y_scales", align_bytes=64)
+
+        def y_job(c, h):
+            def run(tick):
+                bank = bank_tile()
+                for g in range(GROUPS):
+                    matmul(bank[:], window(positions[g, c], 0, P), window(drag[g, h], 0, PASS), g == 0, g == GROUPS - 1)
+                cols = slice(h * PASS, (h + 1) * PASS)
+                total = stage.tile([P, PASS], F32, name="total", bufs=3)
+                y = stage.tile([P, PASS], F32, name="y", bufs=4)
+                words = stage.tile([P, PASS], BF16, name="y_bf16", bufs=6)
+                y_words[c, h] = words
+
+                def add():
+                    nc.vector.tensor_tensor(out=total[:], in0=bank[:], in1=small["views"][:, c, cols], op=ALU.add)
+
+                def scale():
+                    nc.vector.tensor_tensor(out=y[:], in0=total[:], in1=small["aversion"][:, cols], op=ALU.mult)
+                    nc.sync.dma_start(out=out_0[c * P:(c + 1) * P, cols], in_=y[:])
+
+                def round_words():
+                    nc.scalar.copy(
+                        out=words[:].rearrange("p (u m e) -> p u m e", u=2, e=2),
+                        in_=y[:].rearrange("p (m u e) -> p u m e", u=2, e=2),
+                    )
+                after(tick, Y_ADD, add)
+                after(tick, Y_MUL, scale)
+                after(tick, Y_CAST, round_words)
+            jobs.append(run)
+
+        def planes_job(c, h):
+            def run(tick):
+                bank = bank_tile()
+                for u in range(2):
+                    nc.tensor.transpose(bank[:, u * P:(u + 1) * P], y_words[c, h][:].bitcast(F32)[:, u * P:(u + 1) * P], ident[:])
+                turned = stage.tile([P, PASS], BF16, name="y_turned", align_bytes=64)
+                nc.scalar.copy(
+                    out=turned[:].bitcast(F32).rearrange("p (m u) -> p m u", u=2),
+                    in_=bank[:, : 2 * P].rearrange("p (u m) -> p m u", u=2),
+                )
+                books = slice(c * P, (c + 1) * P)
+
+                def finish():
+                    quantize((y_codes[h][:, books], y_scales[:, h, books]), turned[:])
+                    nc.sync.dma_start(
+                        out=out_1[h].rearrange("p m t -> p (m t)").bitcast(I32)[:, books],
+                        in_=y_codes[h][:, books].bitcast(I32),
+                    )
+                after(tick, 1, finish)
+            jobs.append(run)
+
+        def weave(name, g, run_length, matmul_jobs):
+            units = 2 * passes[name]
+            runs = units // run_length
+            share = len(matmul_jobs) // runs
+            for r in range(runs):
+                for unit in range(r * run_length, (r + 1) * run_length):
+                    transpose_job(name, g, unit)
+                for job, args in matmul_jobs[r * share:(r + 1) * share]:
+                    job(*args)
+
+        def drag_jobs(g, h):
+            return [(drag_job, (g, h, c)) for c in range(PACK)]
+
+        def positions_jobs(g):
+            return [(positions_job, (g, c)) for c in range(CHUNKS)]
+
+        last = GROUPS - 1
+        for a in range(GROUPS):
+            interleave(("directions", 0, a), 2 * a + 1, "vector")
+        weave("risk", 0, 6, [])
+        weave("risk", 1, 3, drag_jobs(0, 0))
+        interleave(("directions", 1, 0), len(jobs) - 1, "vector")
+        interleave(("directions", 1, 1), len(jobs) + 4, "vector")
+        weave("risk", 2, 3, drag_jobs(1, 0))
+        interleave(("directions", 1, 2), len(jobs), "vector")
+        interleave(("alpha", 0, 0), len(jobs) + 6, ENG_A)
+        interleave(("alpha", 0, 1), len(jobs) + 13, "vector")
+        weave("signals", 0, 4, drag_jobs(2, 0) + drag_jobs(0, 1))
+        interleave(("alpha", 0, 2), len(jobs) + 6, ENG_A)
+        interleave(("alpha", 0, 3), len(jobs) + 13, "vector")
+        weave("signals", 1, 4, drag_jobs(1, 1) + drag_jobs(2, 1))
+        if PLAN == 0:
+            weave("signals", 2, 4, positions_jobs(0) + positions_jobs(1))
+            positions_job(last, 0)
+            positions_job(last, 1)
+            for c in range(CHUNKS + TY_LAG):
+                if c < CHUNKS:
+                    y_job(c, 0)
+                    y_job(c, 1)
+                if c + 2 < CHUNKS:
+                    positions_job(last, c + 2)
+                if c >= TY_LAG:
+                    planes_job(c - TY_LAG, 0)
+                    planes_job(c - TY_LAG, 1)
+        else:
+            weave("signals", 2, 4, [(positions_job, (g, c)) for c in range(2) for g in range(2)])
+            positions_job(last, 0)
+            positions_job(last, 1)
+            for c in range(CHUNKS + TY_LAG):
+                if c < CHUNKS:
+                    y_job(c, 0)
+                    y_job(c, 1)
+                if c + 2 < CHUNKS:
+                    for g in range(GROUPS):
+                        positions_job(g, c + 2)
+                if c >= TY_LAG:
+                    planes_job(c - TY_LAG, 0)
+                    planes_job(c - TY_LAG, 1)
+
+        for tick in range(len(jobs) + 4):
+            for lag, task in sorted(later[tick], key=lambda entry: entry[0]):
+                task()
+            if tick < len(jobs):
+                jobs[tick](tick)
+
+        scale_rows = out_2.bitcast(I32).rearrange("h q m -> q h m")
+        for quadrant in range(4):
+            queue = nc.sync if quadrant % 2 == 0 else nc.scalar
+            queue.dma_start(
+                out=scale_rows[4 * quadrant: 4 * quadrant + 4],
+                in_=y_scales[32 * quadrant: 32 * quadrant + 4].bitcast(I32),
+            )

@@ -22,15 +22,30 @@ PASS = P * PACK
 GROUPS = A // PASS
 CHUNKS = B // P
 HALVES = D // PASS
-RAW_BUFS = 10
+RAW_BUFS = 9
 SORT_LEAD = 5
-QUANT_LAG = 2
+QUANT_LAG = 4
 SORT_FROM = 2
-Y_ADD, Y_MUL, Y_CAST = 1, 2, 3
-P_MUL, P_Q = 1, 2
-T_LAG = 2
+Y_ADD, Y_MUL, Y_CAST = 1, 2, 6
+P_MUL, P_Q = 2, 3
+T_LAG = 4
+SORT_S = ()
+WARM0 = 24
+WARM1 = 6
+I1, I2, I3, I4, I5 = 1, 3, 5, 6, 4
+D1 = 0
 PLAN = 1
-ORD = 0
+ORD = 1
+END = "W30 R00 R01 W06 R02 R03 W06 R04 R05 R10 R11 D00 D01 R12 R13 R14 R15 D10 D11 R20 R21 R22 D02 D03 R23 R24 R25 D12 D13 S00 S01 S02 S03 D20 D21 D22 D23 S04 S05 S06 S07 D04 D05 D06 D07 S10 S11 S12 S13 D14 D15 D16 D17 S14 S15 S16 S17 D24 D25 D26 D27 S20 S21 S22 S23 P00 P10 S24 S25 S26 S27 P01 P11 P20 P21 P02 P12 Y00 P22 Y01 P03 Y10 P13 Y11 P23 Y20 T00 T01 T10 T11 Y21 Y30 Z31 T20 T21 T30 T31"
+LOOK = 4
+H0 = 0
+FILL = [1, 3, 6, 12, 14, 18, 22, 28, 34, 42, 48, 54, 60]
+SL = [1, 1, 5, 5, 5]
+SPLIT = 1
+UNSORTED = 8
+LOADS = "r00 d00 r01 d01 r02 d02 r03 r10 r11 r12 r13 d10 d11 d12 r20 r21 r22 r23 d20 d21 d22 s00 s01 s02 s03 a00 a01 a02 a03 s10 s11 s12 s13 s20 s21 s22 s23"
+RUNT = 2
+SPC = 0
 TY_LAG=2
 ENG_A = "vector"
 
@@ -72,16 +87,9 @@ def tile_book_risk_drag_h3_kernel(
 
         row_major = {"risk": risk, "signals": signals}
         passes = {"risk": A // PASS, "signals": K // PASS}
-        order = []
-        for t in range(PACK):
-            order.append(("risk", 0, t))
-            if t < GROUPS:
-                order.append(("directions", 0, t))
-        order.extend(("risk", g, t) for g in (1, 2) for t in range(PACK))
-        order.extend(("directions", 1, a) for a in range(GROUPS))
-        order.extend(("signals", 0, t) for t in range(PACK))
-        order.extend(("alpha", 0, a) for a in range(passes["signals"]))
-        order.extend(("signals", g, t) for g in (1, 2) for t in range(PACK))
+        strips = {"directions": [(0, 2), (2, 2), (4, 4)], "alpha": [(0, 4)]}
+        names = {"r": "risk", "d": "directions", "s": "signals", "a": "alpha"}
+        order = [(names[w[0]], int(w[1]), int(w[2])) for w in LOADS.split()]
         raw = {}
         consumed = set()
         small = {}
@@ -94,8 +102,9 @@ def tile_book_risk_drag_h3_kernel(
                 nc.sync.dma_start(out=tile[:], in_=src)
             else:
                 matrix = directions if name == "directions" else alpha
-                src = matrix[j * PASS:(j + 1) * PASS, i * PASS:(i + 1) * PASS].rearrange("(p t) n -> p t n", t=PACK)
-                tile = raw_pool.tile([P, PACK, PASS], BF16, name="raw")
+                first, count = strips[name][i]
+                src = matrix[j * PASS:(j + 1) * PASS, first * P:(first + count) * P].rearrange("(p t) n -> p t n", t=PACK)
+                tile = raw_pool.tile([P, PACK, count * P], BF16, name="raw")
                 nc.sync.dma_start(out=tile[:], in_=src)
             raw[key] = tile
 
@@ -129,14 +138,26 @@ def tile_book_risk_drag_h3_kernel(
         later = defaultdict(list)
         jobs = []
 
-        def after(tick, lag, task):
-            later[tick + lag].append((lag * ORD, task))
+        pending = {}
+        needs = defaultdict(list)
+
+        def after(tick, lag, task, key=None):
+            if key is None:
+                later[tick + lag].append((lag * ORD, task))
+            else:
+                pending[key] = task
+                later[tick + lag].append((lag * ORD, lambda: ensure(key)))
+
+        def ensure(key):
+            if key in pending:
+                pending.pop(key)()
 
         moving = {}
 
         def interleave(key, tick, engine):
             def copy():
-                grouped = stage.tile([P, PASS, PACK], BF16, name="grouped", bufs=2, align_bytes=64)
+                width = strips[key[0]][key[1]][1] * P
+                grouped = stage.tile([P, width, PACK], BF16, name="grouped", bufs=2, align_bytes=64)
                 dst = grouped[:].rearrange("p (c i) t -> p c t i", i=4)
                 src = raw[key][:].rearrange("p t (c i) -> p c t i", i=4)
                 if engine == "vector":
@@ -144,8 +165,11 @@ def tile_book_risk_drag_h3_kernel(
                 else:
                     nc.scalar.copy(out=dst, in_=src)
                 release(key)
-                moving[key] = mx_tiles("%s_%d_%d" % key, PASS)
-                after(tick, 1, lambda: quantize(window(moving[key], 0, PASS), grouped[:].rearrange("p n t -> p (n t)")))
+                mx = mx_tiles("%s_%d_%d" % key, width)
+                first, count = strips[key[0]][key[1]]
+                for c in range(count):
+                    moving[key[0], first + c, key[2]] = window(mx, c, P)
+                after(tick, 1, lambda: quantize(window(mx, 0, width), grouped[:].rearrange("p n t -> p (n t)")), ("q",) + key)
             after(tick, 0, copy)
 
         sorted_words = {}
@@ -153,32 +177,37 @@ def tile_book_risk_drag_h3_kernel(
 
         def sort_words(key):
             n_pass = passes[key[0]]
-            tile = stage.tile([P, 2, n_pass, P], F32, name="sorted", bufs=4)
-            nc.vector.tensor_copy(out=tile[:], in_=raw[key][:].bitcast(F32).rearrange("p (a m u) -> p u a m", m=P, u=2))
+            tile = stage.tile([P, 2, n_pass, P], F32, name="sorted", bufs=5)
+            src = raw[key][:].bitcast(F32).rearrange("p (a m u) -> p u a m", m=P, u=2)
+            if key[2] in SORT_S:
+                nc.scalar.copy(out=tile[:], in_=src)
+            else:
+                nc.vector.tensor_copy(out=tile[:], in_=src)
             release(key)
             sorted_words[key] = tile
 
         def transpose_job(name, g, unit):
             n_pass = passes[name]
             pairs = [divmod(n, n_pass) for n in (2 * unit, 2 * unit + 1)]
-            is_sorted = name == "signals" or g >= SORT_FROM
-            if is_sorted:
+            def is_sorted(t):
+                return name == "signals" or PACK * g + t >= UNSORTED
+            if True:
                 for t, a in pairs:
-                    if a == 0:
-                        after(len(jobs) - SORT_LEAD, 0, lambda t=t: sort_words((name, g, t)))
+                    if a == 0 and is_sorted(t):
+                        after(len(jobs) - SL[g - 1 if name == "risk" else 2 + g] - (t % RUNT) * SPC, 0, lambda t=t: sort_words((name, g, t)))
 
             def run(tick):
                 bank = bank_tile()
                 for i, (t, a) in enumerate(pairs):
                     for u in range(2):
-                        if is_sorted:
+                        if is_sorted(t):
                             src = sorted_words[name, g, t][:, u, a, :]
                         else:
                             src = raw[name, g, t][:].bitcast(F32)[:, 2 * P * a + u: 2 * P * (a + 1): 2]
                         nc.tensor.transpose(bank[:, (2 * i + u) * P:(2 * i + u + 1) * P], src, ident[:])
-                    if not is_sorted and a == n_pass - 1:
+                    if not is_sorted(t) and a == n_pass - 1:
                         release((name, g, t))
-                turned = stage.tile([P, 2 * PASS], BF16, name="turned", bufs=4, align_bytes=64)
+                turned = stage.tile([P, 2 * PASS], BF16, name="turned", bufs=T_LAG + 2, align_bytes=64)
                 nc.scalar.copy(
                     out=turned[:].bitcast(F32).rearrange("p (i m u) -> p i m u", i=2, u=2),
                     in_=bank[:].rearrange("p (i u m) -> p i m u", i=2, u=2),
@@ -189,7 +218,7 @@ def tile_book_risk_drag_h3_kernel(
                     mx = mx_tiles("signals_%d_%d" % (g, unit), 2 * P, pool=stage, tag="signals", bufs=24)
                 for i, (t, a) in enumerate(pairs):
                     stationary[name, g, t, a] = window(mx, i, P)
-                after(tick, T_LAG, lambda: quantize(window(mx, 0, 2 * P), turned[:]))
+                after(tick, T_LAG, lambda: quantize(window(mx, 0, 2 * P), turned[:]), (name, g, unit))
             jobs.append(run)
 
         drag = {(g, h): mx_tiles("drag_%d_%d" % (g, h), PASS) for g in range(GROUPS) for h in range(HALVES)}
@@ -198,30 +227,36 @@ def tile_book_risk_drag_h3_kernel(
         def first_stage(bank, name, partner, g, h, c):
             for t in range(PACK):
                 for a in range(passes[name]):
-                    matmul(bank[:, t * P:(t + 1) * P], stationary[name, g, t, a], window(moving[partner, h, a], c, P),
+                    matmul(bank[:, t * P:(t + 1) * P], stationary[name, g, t, a], moving[partner, PACK * h + c, a],
                            a == 0, a == passes[name] - 1)
 
         def drag_job(g, h, c):
+            needs[len(jobs)].extend([("risk", g, u) for u in range(6)] + [("q", "directions", j, a) for j in range(3) for a in range(3) if strips["directions"][j][0] <= PACK * h + c < sum(strips["directions"][j])])
             def run(tick):
                 bank = bank_tile()
                 first_stage(bank, "risk", "directions", g, h, c)
-                rounded = stage.tile([P, P, PACK], BF16, name="drag_bf16", bufs=4, align_bytes=64)
+                rounded = stage.tile([P, P, PACK], BF16, name="drag_bf16", bufs=QUANT_LAG + 2, align_bytes=64)
                 nc.scalar.activation(out=rounded[:], in_=bank[:].rearrange("p (t n) -> p n t", t=PACK), func=ACT.Copy, scale=-1.0)
-                after(tick, QUANT_LAG, lambda: quantize(window(drag[g, h], c, P), rounded[:].rearrange("p n t -> p (n t)")))
+                after(tick, QUANT_LAG, lambda: quantize(window(drag[g, h], c, P), rounded[:].rearrange("p n t -> p (n t)")), ("drag", g, h, c))
             jobs.append(run)
 
         def positions_job(g, c):
+            needs[len(jobs)].extend([("signals", g, u) for u in range(8)] + [("q", "alpha", 0, a) for a in range(4)])
             def run(tick):
                 bank = bank_tile()
                 first_stage(bank, "signals", "alpha", g, 0, c)
-                squashed = stage.tile([P, P, PACK], F32, name="squashed")
+                squashed = stage.tile([P, P, PACK], F32, name="squashed", bufs=P_MUL + 2)
                 nc.scalar.activation(out=squashed[:], in_=bank[:].rearrange("p (t n) -> p n t", t=PACK), func=ACT.Tanh)
-                rounded = stage.tile([P, P, PACK], BF16, name="positions_bf16", align_bytes=64)
+                rounded = stage.tile([P, P, PACK], BF16, name="positions_bf16", bufs=P_Q + 1, align_bytes=64)
                 positions[g, c] = mx_tiles("positions_%d_%d" % (g, c), P)
                 after(tick, P_MUL, lambda: nc.vector.tensor_tensor(
                     out=rounded[:], in0=squashed[:],
-                    in1=small["limit"][:, g, :].unsqueeze(1).to_broadcast([P, P, PACK]), op=ALU.mult))
-                after(tick, P_Q, lambda: quantize(window(positions[g, c], 0, P), rounded[:].rearrange("p n t -> p (n t)")))
+                    in1=small["limit"][:, g, :].unsqueeze(1).to_broadcast([P, P, PACK]), op=ALU.mult), ("limited", g, c))
+
+                def finish():
+                    ensure(("limited", g, c))
+                    quantize(window(positions[g, c], 0, P), rounded[:].rearrange("p n t -> p (n t)"))
+                after(tick, P_Q, finish, ("positions", g, c))
             jobs.append(run)
 
         y_words = {}
@@ -229,6 +264,7 @@ def tile_book_risk_drag_h3_kernel(
         y_scales = keep.tile([P, HALVES, B], U8, name="y_scales", align_bytes=64)
 
         def y_job(c, h):
+            needs[len(jobs)].extend([("positions", g, c) for g in range(3)] + [("drag", g, h, i) for g in range(3) for i in range(4)])
             def run(tick):
                 bank = bank_tile()
                 for g in range(GROUPS):
@@ -243,20 +279,69 @@ def tile_book_risk_drag_h3_kernel(
                     nc.vector.tensor_tensor(out=total[:], in0=bank[:], in1=small["views"][:, c, cols], op=ALU.add)
 
                 def scale():
+                    ensure(("add", c, h))
                     nc.vector.tensor_tensor(out=y[:], in0=total[:], in1=small["aversion"][:, cols], op=ALU.mult)
                     nc.sync.dma_start(out=out_0[c * P:(c + 1) * P, cols], in_=y[:])
 
                 def round_words():
+                    ensure(("scale", c, h))
                     nc.scalar.copy(
                         out=words[:].rearrange("p (u m e) -> p u m e", u=2, e=2),
                         in_=y[:].rearrange("p (m u e) -> p u m e", u=2, e=2),
                     )
-                after(tick, Y_ADD, add)
-                after(tick, Y_MUL, scale)
-                after(tick, Y_CAST, round_words)
+                after(tick, Y_ADD, add, ("add", c, h))
+                after(tick, Y_MUL, scale, ("scale", c, h))
+                after(tick, Y_CAST, round_words, ("words", c, h))
             jobs.append(run)
 
+        def last_y_jobs(c, h):
+            cols = slice(h * PASS, (h + 1) * PASS)
+            tiles = {}
+
+            def piece(i):
+                half = slice(i * 2 * P, (i + 1) * 2 * P)
+                needs[len(jobs)].extend([("positions", g, c) for g in range(3)])
+
+                def run(tick):
+                    bank = bank_tile()
+                    for g in range(GROUPS):
+                        matmul(bank[:, : 2 * P], window(positions[g, c], 0, P), window(drag[g, h], i, 2 * P), g == 0, g == GROUPS - 1)
+                    if i == 0:
+                        tiles["total"] = stage.tile([P, PASS], F32, name="total", bufs=3)
+                        tiles["y"] = stage.tile([P, PASS], F32, name="y", bufs=4)
+                        y_words[c, h] = stage.tile([P, PASS], BF16, name="y_bf16", bufs=6)
+                    total = tiles["total"]
+
+                    def add():
+                        nc.vector.tensor_tensor(out=total[:, half], in0=bank[:, : 2 * P], in1=small["views"][:, c, cols][:, half], op=ALU.add)
+
+                    def words():
+                        ensure(("add", c, h, i))
+                        nc.vector.tensor_tensor(
+                            out=y_words[c, h][:].rearrange("p (u m e) -> p u m e", u=2, e=2)[:, :, i * 64:(i + 1) * 64, :],
+                            in0=total[:, half].rearrange("p (m u e) -> p u m e", u=2, e=2),
+                            in1=small["aversion"][:, cols][:, half].rearrange("p (m u e) -> p u m e", u=2, e=2), op=ALU.mult)
+
+                    def both():
+                        ensure(("add", c, h, 1))
+                        ensure(("piece", c, h, 0))
+                        words()
+
+                    def scale():
+                        nc.vector.tensor_tensor(out=tiles["y"][:], in0=total[:], in1=small["aversion"][:, cols], op=ALU.mult)
+                        nc.sync.dma_start(out=out_0[c * P:(c + 1) * P, cols], in_=tiles["y"][:])
+                    after(tick, 1, add, ("add", c, h, i))
+                    if i == 0:
+                        after(tick, 3, words, ("piece", c, h, 0))
+                    else:
+                        after(tick, 2, both, ("words", c, h))
+                        after(tick, 3, scale)
+                jobs.append(run)
+            piece(0)
+            piece(1)
+
         def planes_job(c, h):
+            needs[len(jobs)].append(("words", c, h))
             def run(tick):
                 bank = bank_tile()
                 for u in range(2):
@@ -293,52 +378,41 @@ def tile_book_risk_drag_h3_kernel(
         def positions_jobs(g):
             return [(positions_job, (g, c)) for c in range(CHUNKS)]
 
-        last = GROUPS - 1
-        for a in range(GROUPS):
-            interleave(("directions", 0, a), 2 * a + 1, "vector")
-        weave("risk", 0, 6, [])
-        weave("risk", 1, 3, drag_jobs(0, 0))
-        interleave(("directions", 1, 0), len(jobs) - 1, "vector")
-        interleave(("directions", 1, 1), len(jobs) + 4, "vector")
-        weave("risk", 2, 3, drag_jobs(1, 0))
-        interleave(("directions", 1, 2), len(jobs), "vector")
-        interleave(("alpha", 0, 0), len(jobs) + 6, ENG_A)
-        interleave(("alpha", 0, 1), len(jobs) + 13, "vector")
-        weave("signals", 0, 4, drag_jobs(2, 0) + drag_jobs(0, 1))
-        interleave(("alpha", 0, 2), len(jobs) + 6, ENG_A)
-        interleave(("alpha", 0, 3), len(jobs) + 13, "vector")
-        weave("signals", 1, 4, drag_jobs(1, 1) + drag_jobs(2, 1))
-        if PLAN == 0:
-            weave("signals", 2, 4, positions_jobs(0) + positions_jobs(1))
-            positions_job(last, 0)
-            positions_job(last, 1)
-            for c in range(CHUNKS + TY_LAG):
-                if c < CHUNKS:
-                    y_job(c, 0)
-                    y_job(c, 1)
-                if c + 2 < CHUNKS:
-                    positions_job(last, c + 2)
-                if c >= TY_LAG:
-                    planes_job(c - TY_LAG, 0)
-                    planes_job(c - TY_LAG, 1)
-        else:
-            weave("signals", 2, 4, [(positions_job, (g, c)) for c in range(2) for g in range(2)])
-            positions_job(last, 0)
-            positions_job(last, 1)
-            for c in range(CHUNKS + TY_LAG):
-                if c < CHUNKS:
-                    y_job(c, 0)
-                    y_job(c, 1)
-                if c + 2 < CHUNKS:
-                    for g in range(GROUPS):
-                        positions_job(g, c + 2)
-                if c >= TY_LAG:
-                    planes_job(c - TY_LAG, 0)
-                    planes_job(c - TY_LAG, 1)
+        warm_bf16 = keep.tile([P, PASS], BF16, name="warm_bf16", align_bytes=64)
+        warm = window(mx_tiles("warm", P), 0, P)
+        nc.vector.memset(warm_bf16[:], 0.0)
+        quantize(warm, warm_bf16[:])
 
-        for tick in range(len(jobs) + 4):
+        def warm_job(count):
+            def run(tick):
+                bank = bank_tile()
+                for i in range(count):
+                    matmul(bank[:, :P], warm, warm, True, True)
+            if count:
+                jobs.append(run)
+
+        keys = [("directions", j, a) for j in range(3) for a in range(3)] + [("alpha", 0, a) for a in range(4)]
+        for key, tick in zip(keys, FILL):
+            interleave(key, tick, "vector")
+        for word in END.split():
+            kind, i, j = word[0], int(word[1]), int(word[2])
+            if kind == "W":
+                warm_job(10 * i + j)
+            elif kind == "R":
+                transpose_job("risk", i, j)
+            elif kind == "S":
+                transpose_job("signals", i, j)
+            elif kind == "D":
+                drag_job(i, j // 4, j % 4)
+            else:
+                {"P": positions_job, "Y": y_job, "T": planes_job, "Z": last_y_jobs}[kind](i, j)
+
+        for tick in range(len(jobs) + 8):
             for lag, task in sorted(later[tick], key=lambda entry: entry[0]):
                 task()
+            for ahead in range(LOOK + 1):
+                for key in needs[tick + ahead]:
+                    ensure(key)
             if tick < len(jobs):
                 jobs[tick](tick)
 

@@ -20,34 +20,16 @@ P = 128
 PACK = 4
 PASS = P * PACK
 GROUPS = A // PASS
-CHUNKS = B // P
+BOOK_CHUNKS = B // P
 HALVES = D // PASS
+PASSES = {"risk": A // PASS, "signals": K // PASS}
+STRIPS = {"directions": [(0, 2), (2, 2), (4, 4)], "alpha": [(0, 4)]}
+
+LAG = 4
+UNSORTED_GROUPS = 2
+WARM_FIRST, WARM_BETWEEN = 30, 6
 RAW_BUFS = 9
-SORT_LEAD = 5
-QUANT_LAG = 4
-SORT_FROM = 2
-Y_ADD, Y_MUL, Y_CAST = 1, 2, 6
-P_MUL, P_Q = 2, 3
-T_LAG = 4
-SORT_S = ()
-WARM0 = 24
-WARM1 = 6
-I1, I2, I3, I4, I5 = 1, 3, 5, 6, 4
-D1 = 0
-PLAN = 1
-ORD = 1
-END = "W30 R00 R01 W06 R02 R03 W06 R04 R05 R10 R11 D00 D01 R12 R13 R14 R15 D10 D11 R20 R21 R22 D02 D03 R23 R24 R25 D12 D13 S00 S01 S02 S03 D20 D21 D22 D23 S04 S05 S06 S07 D04 D05 D06 D07 S10 S11 S12 S13 D14 D15 D16 D17 S14 S15 S16 S17 D24 D25 D26 D27 S20 S21 S22 S23 P00 P10 S24 S25 S26 S27 P01 P11 P20 P21 P02 P12 Y00 P22 Y01 P03 Y10 P13 Y11 P23 Y20 T00 T01 T10 T11 Y21 Y30 Z31 T20 T21 T30 T31"
-LOOK = 4
-H0 = 0
-FILL = [1, 3, 6, 12, 14, 18, 22, 28, 34, 42, 48, 54, 60]
-SL = [1, 1, 5, 5, 5]
-SPLIT = 1
-UNSORTED = 8
-LOADS = "r00 d00 r01 d01 r02 d02 r03 r10 r11 r12 r13 d10 d11 d12 r20 r21 r22 r23 d20 d21 d22 s00 s01 s02 s03 a00 a01 a02 a03 s10 s11 s12 s13 s20 s21 s22 s23"
-RUNT = 2
-SPC = 0
-TY_LAG=2
-ENG_A = "vector"
+TURNED_BUFS = 16
 
 
 def tile_book_risk_drag_h3_kernel(
@@ -64,10 +46,10 @@ def tile_book_risk_drag_h3_kernel(
         ident = keep.tile([P, P], F32, name="ident")
         make_identity(nc, ident[:])
 
-        def mx_tiles(name, width, pool=keep, tag=None, bufs=None):
-            codes = pool.tile([P, width], U32, name=name + "_codes", tag=(tag or name) + "_codes", bufs=bufs, align_bytes=64)
-            scales = pool.tile([P, width], U8, name=name + "_scales", tag=(tag or name) + "_scales", bufs=bufs, align_bytes=64)
-            return codes, scales
+        def mx_tiles(name, width, pool=keep, bufs=None):
+            codes = pool.tile([P, width], U32, name=name + "_codes", bufs=bufs, align_bytes=64)
+            scales = pool.tile([P, width], U8, name=name + "_scales", bufs=bufs, align_bytes=64)
+            return codes[:], scales[:]
 
         def window(mx, i, width):
             cols = slice(i * width, (i + 1) * width)
@@ -85,49 +67,51 @@ def tile_book_risk_drag_h3_kernel(
         def bank_tile():
             return psum.tile([P, PASS], F32, name="bank")
 
-        row_major = {"risk": risk, "signals": signals}
-        passes = {"risk": A // PASS, "signals": K // PASS}
-        strips = {"directions": [(0, 2), (2, 2), (4, 4)], "alpha": [(0, 4)]}
-        names = {"r": "risk", "d": "directions", "s": "signals", "a": "alpha"}
-        order = [(names[w[0]], int(w[1]), int(w[2])) for w in LOADS.split()]
+        def slots_of(name, g):
+            return [(name, g, t) for t in range(PACK)]
+
+        def passes_of(name, s):
+            partner = "risk" if name == "directions" else "signals"
+            return [(name, s, a) for a in range(PASSES[partner])]
+
+        def alternate(first, second):
+            mixed = [key for both in zip(first, second) for key in both]
+            return mixed + first[len(second):] + second[len(first):]
+
+        order = (
+            alternate(slots_of("risk", 0), passes_of("directions", 0))
+            + slots_of("risk", 1) + passes_of("directions", 1) + slots_of("risk", 2)
+            + alternate(passes_of("directions", 2), slots_of("signals", 0))
+            + alternate(passes_of("alpha", 0), slots_of("signals", 1))
+            + slots_of("signals", 2)
+        )
+        inputs = {"risk": risk, "signals": signals, "directions": directions, "alpha": alpha}
         raw = {}
         consumed = set()
-        small = {}
+        limit_sb = keep.tile([P, GROUPS, PACK], BF16, name="limit_sb")
+        views_sb = keep.tile([P, BOOK_CHUNKS, D], BF16, name="views_sb")
+        aversion_sb = keep.tile([P, D], BF16, name="aversion_sb")
 
         def load(key):
             name, i, j = key
-            if name in row_major:
-                src = row_major[name][i * PASS:(i + 1) * PASS, :].rearrange("(m t) k -> m t k", t=PACK)[:, j, :]
-                tile = raw_pool.tile([P, passes[name] * PASS], BF16, name="raw")
-                nc.sync.dma_start(out=tile[:], in_=src)
+            if name in PASSES:
+                src = inputs[name][i * PASS:(i + 1) * PASS, :].rearrange("(m t) k -> m t k", t=PACK)[:, j, :]
+                raw[key] = raw_pool.tile([P, PASSES[name] * PASS], BF16, name="raw")
             else:
-                matrix = directions if name == "directions" else alpha
-                first, count = strips[name][i]
-                src = matrix[j * PASS:(j + 1) * PASS, first * P:(first + count) * P].rearrange("(p t) n -> p t n", t=PACK)
-                tile = raw_pool.tile([P, PACK, count * P], BF16, name="raw")
-                nc.sync.dma_start(out=tile[:], in_=src)
-            raw[key] = tile
-
-        def load_small():
-            small["limit"] = keep.tile([P, GROUPS, PACK], BF16, name="limit_sb")
-            nc.sync.dma_start(out=small["limit"][:], in_=limit.rearrange("(g p t) -> p g t", p=P, t=PACK))
-
-        def load_last():
-            small["views"] = keep.tile([P, CHUNKS, D], BF16, name="views_sb")
-            nc.sync.dma_start(out=small["views"][:], in_=views.rearrange("(c p) d -> p c d", p=P))
-            small["aversion"] = keep.tile([P, D], BF16, name="aversion_sb")
-            nc.sync.dma_start(out=small["aversion"][:], in_=aversion.partition_broadcast(P))
+                first, count = STRIPS[name][i]
+                rows = inputs[name][j * PASS:(j + 1) * PASS, first * P:(first + count) * P]
+                src = rows.rearrange("(p t) n -> p t n", t=PACK)
+                raw[key] = raw_pool.tile([P, PACK, count * P], BF16, name="raw")
+            nc.sync.dma_start(out=raw[key][:], in_=src)
+            if key == ("alpha", 0, 0):
+                nc.sync.dma_start(out=limit_sb[:], in_=limit.rearrange("(g p t) -> p g t", p=P, t=PACK))
+            if key == order[-1]:
+                nc.sync.dma_start(out=views_sb[:], in_=views.rearrange("(c p) d -> p c d", p=P))
+                nc.sync.dma_start(out=aversion_sb[:], in_=aversion.partition_broadcast(P))
 
         def issue_loads():
-            while len(raw) < len(order):
-                n = len(raw)
-                if n >= RAW_BUFS and any(key not in consumed for key in order[: n - RAW_BUFS + 1]):
-                    return
-                load(order[n])
-                if order[n] == ("alpha", 0, 0):
-                    load_small()
-                if n + 1 == len(order):
-                    load_last()
+            while len(raw) < len(order) and all(key in consumed for key in order[: max(0, len(raw) - RAW_BUFS + 1)]):
+                load(order[len(raw)])
 
         def release(key):
             consumed.add(key)
@@ -135,286 +119,346 @@ def tile_book_risk_drag_h3_kernel(
 
         issue_loads()
 
-        later = defaultdict(list)
         jobs = []
-
-        pending = {}
         needs = defaultdict(list)
+        due = defaultdict(list)
+        pending = {}
 
-        def after(tick, lag, task, key=None):
-            if key is None:
-                later[tick + lag].append((lag * ORD, task))
-            else:
-                pending[key] = task
-                later[tick + lag].append((lag * ORD, lambda: ensure(key)))
+        def after(number, distance, name, step):
+            pending[name] = step
+            due[number + distance].append((distance, name))
 
-        def ensure(key):
-            if key in pending:
-                pending.pop(key)()
+        def ensure(name):
+            if name in pending:
+                pending.pop(name)()
 
         moving = {}
 
-        def interleave(key, tick, engine):
+        def interleave(key):
+            name, s, a = key
+            first, count = STRIPS[name][s]
+            number = len(jobs)
+
             def copy():
-                width = strips[key[0]][key[1]][1] * P
-                grouped = stage.tile([P, width, PACK], BF16, name="grouped", bufs=2, align_bytes=64)
-                dst = grouped[:].rearrange("p (c i) t -> p c t i", i=4)
-                src = raw[key][:].rearrange("p t (c i) -> p c t i", i=4)
-                if engine == "vector":
-                    nc.vector.tensor_copy(out=dst, in_=src)
-                else:
-                    nc.scalar.copy(out=dst, in_=src)
+                grouped = stage.tile([P, count * P, PACK], BF16, name="grouped", bufs=2, align_bytes=64)
+                nc.vector.tensor_copy(
+                    out=grouped[:].rearrange("p (c i) t -> p c t i", i=4),
+                    in_=raw[key][:].rearrange("p t (c i) -> p c t i", i=4),
+                )
                 release(key)
-                mx = mx_tiles("%s_%d_%d" % key, width)
-                first, count = strips[key[0]][key[1]]
-                for c in range(count):
-                    moving[key[0], first + c, key[2]] = window(mx, c, P)
-                after(tick, 1, lambda: quantize(window(mx, 0, width), grouped[:].rearrange("p n t -> p (n t)")), ("q",) + key)
-            after(tick, 0, copy)
+                mx = mx_tiles("%s_%d_%d" % key, count * P)
+                for chunks in (1, 2):
+                    for c in range(0, count, chunks):
+                        moving[name, first + c, chunks, a] = window(mx, c // chunks, chunks * P)
+                after(number, 1, key, lambda: quantize(mx, grouped[:].rearrange("p n t -> p (n t)")))
 
-        sorted_words = {}
+            after(number, 0, ("interleave",) + key, copy)
+
+        def strip_passes(name, chunk):
+            s = [first <= chunk < first + count for first, count in STRIPS[name]].index(True)
+            return passes_of(name, s)
+
+        sorted_pairs = {}
         stationary = {}
+        shared = {}
 
-        def sort_words(key):
-            n_pass = passes[key[0]]
-            tile = stage.tile([P, 2, n_pass, P], F32, name="sorted", bufs=5)
-            src = raw[key][:].bitcast(F32).rearrange("p (a m u) -> p u a m", m=P, u=2)
-            if key[2] in SORT_S:
-                nc.scalar.copy(out=tile[:], in_=src)
-            else:
-                nc.vector.tensor_copy(out=tile[:], in_=src)
+        def sort_pairs(key):
+            tile = stage.tile([P, 2, PASSES[key[0]], P], F32, name="sorted", bufs=PACK)
+            nc.vector.tensor_copy(out=tile[:], in_=raw[key][:].bitcast(F32).rearrange("p (a m u) -> p u a m", m=P, u=2))
             release(key)
-            sorted_words[key] = tile
+            sorted_pairs[key] = tile
 
         def transpose_job(name, g, unit):
-            n_pass = passes[name]
-            pairs = [divmod(n, n_pass) for n in (2 * unit, 2 * unit + 1)]
-            def is_sorted(t):
-                return name == "signals" or PACK * g + t >= UNSORTED
-            if True:
-                for t, a in pairs:
-                    if a == 0 and is_sorted(t):
-                        after(len(jobs) - SL[g - 1 if name == "risk" else 2 + g] - (t % RUNT) * SPC, 0, lambda t=t: sort_words((name, g, t)))
+            parts = [divmod(n, PASSES[name]) for n in (2 * unit, 2 * unit + 1)]
+            is_sorted = name == "signals" or g >= UNSORTED_GROUPS
+            merged = 2 if is_sorted else 1
+            lead = LAG if name == "signals" else 1
+            for t, a in parts:
+                if is_sorted and a == 0:
+                    after(len(jobs) - lead, 0, ("sort", name, g, t), lambda t=t: sort_pairs((name, g, t)))
 
-            def run(tick):
+            def run(number):
                 bank = bank_tile()
-                for i, (t, a) in enumerate(pairs):
+                for i, (t, a) in enumerate(parts):
                     for u in range(2):
-                        if is_sorted(t):
-                            src = sorted_words[name, g, t][:, u, a, :]
+                        if is_sorted:
+                            src = sorted_pairs[name, g, t][:, u, a, :]
                         else:
                             src = raw[name, g, t][:].bitcast(F32)[:, 2 * P * a + u: 2 * P * (a + 1): 2]
                         nc.tensor.transpose(bank[:, (2 * i + u) * P:(2 * i + u + 1) * P], src, ident[:])
-                    if not is_sorted(t) and a == n_pass - 1:
+                    if not is_sorted and a == PASSES[name] - 1:
                         release((name, g, t))
-                turned = stage.tile([P, 2 * PASS], BF16, name="turned", bufs=T_LAG + 2, align_bytes=64)
+                part = unit % merged
+                if part == 0:
+                    shared["turned"] = stage.tile([P, merged * 2 * PASS], BF16, name="turned", bufs=LAG, align_bytes=64)
+                if unit % 2 == 0:
+                    shared["turned_mx"] = mx_tiles("turned", 4 * P, pool=stage, bufs=TURNED_BUFS)
+                turned, mx = shared["turned"], shared["turned_mx"]
                 nc.scalar.copy(
-                    out=turned[:].bitcast(F32).rearrange("p (i m u) -> p i m u", i=2, u=2),
+                    out=turned[:, part * 2 * PASS:(part + 1) * 2 * PASS].bitcast(F32).rearrange("p (i m u) -> p i m u", i=2, u=2),
                     in_=bank[:].rearrange("p (i u m) -> p i m u", i=2, u=2),
                 )
-                if name == "risk":
-                    mx = mx_tiles("risk_%d_%d" % (g, unit), 2 * P)
-                else:
-                    mx = mx_tiles("signals_%d_%d" % (g, unit), 2 * P, pool=stage, tag="signals", bufs=24)
-                for i, (t, a) in enumerate(pairs):
-                    stationary[name, g, t, a] = window(mx, i, P)
-                after(tick, T_LAG, lambda: quantize(window(mx, 0, 2 * P), turned[:]), (name, g, unit))
+                for i, (t, a) in enumerate(parts):
+                    stationary[name, g, t, a] = window(mx, 2 * (unit % 2) + i, P)
+                if part == merged - 1:
+                    after(number, LAG, (name, g, unit),
+                          lambda: quantize(window(mx, (unit % 2) // merged, merged * 2 * P), turned[:]))
+
             jobs.append(run)
+
+        def first_stage(bank, name, partner, g, slots, chunk, chunks):
+            width = chunks * P
+            for i, t in enumerate(slots):
+                for a in range(PASSES[name]):
+                    matmul(bank[:, i * width:(i + 1) * width], stationary[name, g, t, a], moving[partner, chunk, chunks, a],
+                           a == 0, a == PASSES[name] - 1)
 
         drag = {(g, h): mx_tiles("drag_%d_%d" % (g, h), PASS) for g in range(GROUPS) for h in range(HALVES)}
+
+        def drag_job(g, chunk):
+            h, c = divmod(chunk, PACK)
+            needs[len(jobs)].extend([("risk", g, unit) for unit in range(2 * PASSES["risk"])] + strip_passes("directions", chunk))
+
+            def run(number):
+                bank = bank_tile()
+                first_stage(bank, "risk", "directions", g, range(PACK), chunk, 1)
+                part = c % 2
+                if part == 0:
+                    shared["drag"] = stage.tile([P, 2 * P, PACK], BF16, name="drag_bf16", align_bytes=64)
+                rounded = shared["drag"]
+                nc.scalar.activation(out=rounded[:, part * P:(part + 1) * P, :], in_=bank[:].rearrange("p (t n) -> p n t", t=PACK),
+                                     func=ACT.Copy, scale=-1.0)
+                if part == 1:
+                    after(number, LAG, ("drag", g, chunk),
+                          lambda: quantize(window(drag[g, h], c // 2, 2 * P), rounded[:].rearrange("p n t -> p (n t)")))
+
+            jobs.append(run)
+
         positions = {}
+        made_by = {}
 
-        def first_stage(bank, name, partner, g, h, c):
-            for t in range(PACK):
-                for a in range(passes[name]):
-                    matmul(bank[:, t * P:(t + 1) * P], stationary[name, g, t, a], moving[partner, PACK * h + c, a],
-                           a == 0, a == passes[name] - 1)
+        def positions_jobs(g, chunk, chunks):
+            per_bank = PACK // chunks
+            width = chunks * P
+            for c in range(chunks):
+                made_by[g, chunk + c] = ("positions", g, chunk)
+            for v in range(chunks):
+                units = range(2 * per_bank * v, 2 * per_bank * (v + 1))
+                needs[len(jobs)].extend([("signals", g, unit) for unit in units] + passes_of("alpha", 0))
 
-        def drag_job(g, h, c):
-            needs[len(jobs)].extend([("risk", g, u) for u in range(6)] + [("q", "directions", j, a) for j in range(3) for a in range(3) if strips["directions"][j][0] <= PACK * h + c < sum(strips["directions"][j])])
-            def run(tick):
-                bank = bank_tile()
-                first_stage(bank, "risk", "directions", g, h, c)
-                rounded = stage.tile([P, P, PACK], BF16, name="drag_bf16", bufs=QUANT_LAG + 2, align_bytes=64)
-                nc.scalar.activation(out=rounded[:], in_=bank[:].rearrange("p (t n) -> p n t", t=PACK), func=ACT.Copy, scale=-1.0)
-                after(tick, QUANT_LAG, lambda: quantize(window(drag[g, h], c, P), rounded[:].rearrange("p n t -> p (n t)")), ("drag", g, h, c))
-            jobs.append(run)
+                def run(number, v=v):
+                    bank = bank_tile()
+                    first_stage(bank, "signals", "alpha", g, range(per_bank * v, per_bank * (v + 1)), chunk, chunks)
+                    if v == 0:
+                        shared["squashed"] = stage.tile([P, chunks, width, per_bank], F32, name="squashed")
+                    squashed = shared["squashed"]
+                    nc.scalar.activation(out=squashed[:, v], in_=bank[:].rearrange("p (u n) -> p n u", u=per_bank), func=ACT.Tanh)
+                    if v < chunks - 1:
+                        return
+                    rounded = stage.tile([P, width, PACK], BF16, name="positions_bf16", align_bytes=64)
+                    mx = mx_tiles("positions_%d_%d" % (g, chunk), width)
+                    for c in range(chunks):
+                        positions[g, chunk + c] = window(mx, c, P)
 
-        def positions_job(g, c):
-            needs[len(jobs)].extend([("signals", g, u) for u in range(8)] + [("q", "alpha", 0, a) for a in range(4)])
-            def run(tick):
-                bank = bank_tile()
-                first_stage(bank, "signals", "alpha", g, 0, c)
-                squashed = stage.tile([P, P, PACK], F32, name="squashed", bufs=P_MUL + 2)
-                nc.scalar.activation(out=squashed[:], in_=bank[:].rearrange("p (t n) -> p n t", t=PACK), func=ACT.Tanh)
-                rounded = stage.tile([P, P, PACK], BF16, name="positions_bf16", bufs=P_Q + 1, align_bytes=64)
-                positions[g, c] = mx_tiles("positions_%d_%d" % (g, c), P)
-                after(tick, P_MUL, lambda: nc.vector.tensor_tensor(
-                    out=rounded[:], in0=squashed[:],
-                    in1=small["limit"][:, g, :].unsqueeze(1).to_broadcast([P, P, PACK]), op=ALU.mult), ("limited", g, c))
+                    def times_limit():
+                        factor = limit_sb[:, g, :].rearrange("p (v u) -> p v u", v=chunks).unsqueeze(1)
+                        nc.vector.tensor_tensor(
+                            out=rounded[:].rearrange("p n (v u) -> p n v u", v=chunks),
+                            in0=squashed[:].rearrange("p v n u -> p n v u"),
+                            in1=factor.to_broadcast([P, width, chunks, per_bank]), op=ALU.mult,
+                        )
 
-                def finish():
-                    ensure(("limited", g, c))
-                    quantize(window(positions[g, c], 0, P), rounded[:].rearrange("p n t -> p (n t)"))
-                after(tick, P_Q, finish, ("positions", g, c))
-            jobs.append(run)
+                    def finish():
+                        ensure(("limit", g, chunk))
+                        quantize(mx, rounded[:].rearrange("p n t -> p (n t)"))
 
-        y_words = {}
+                    after(number, 2, ("limit", g, chunk), times_limit)
+                    after(number, 3, ("positions", g, chunk), finish)
+
+                jobs.append(run)
+
+        y_pairs = {}
         y_codes = [keep.tile([P, B], U32, name="y_codes_%d" % h, align_bytes=64) for h in range(HALVES)]
         y_scales = keep.tile([P, HALVES, B], U8, name="y_scales", align_bytes=64)
 
+        def by_pairs(ap):
+            return ap.rearrange("p (m u e) -> p u m e", u=2, e=2)
+
+        def last_stage(c, h, i, width):
+            bank = bank_tile()
+            for g in range(GROUPS):
+                matmul(bank[:, :width], positions[g, c], window(drag[g, h], i, width), g == 0, g == GROUPS - 1)
+            return bank
+
+        def y_needs(c, h):
+            needs[len(jobs)].extend(
+                [made_by[g, c] for g in range(GROUPS)]
+                + [("drag", g, PACK * h + i) for g in range(GROUPS) for i in range(PACK)]
+            )
+
+        def y_tiles(c, h):
+            total = stage.tile([P, PASS], F32, name="total")
+            y = stage.tile([P, PASS], F32, name="y", bufs=LAG)
+            y_pairs[c, h] = stage.tile([P, PASS], BF16, name="y_bf16", bufs=6)
+            return total, y
+
+        def scale_and_store(c, h, total, y):
+            cols = slice(h * PASS, (h + 1) * PASS)
+            nc.vector.tensor_tensor(out=y[:], in0=total[:], in1=aversion_sb[:, cols], op=ALU.mult)
+            nc.sync.dma_start(out=out_0[c * P:(c + 1) * P, cols], in_=y[:])
+
         def y_job(c, h):
-            needs[len(jobs)].extend([("positions", g, c) for g in range(3)] + [("drag", g, h, i) for g in range(3) for i in range(4)])
-            def run(tick):
-                bank = bank_tile()
-                for g in range(GROUPS):
-                    matmul(bank[:], window(positions[g, c], 0, P), window(drag[g, h], 0, PASS), g == 0, g == GROUPS - 1)
-                cols = slice(h * PASS, (h + 1) * PASS)
-                total = stage.tile([P, PASS], F32, name="total", bufs=3)
-                y = stage.tile([P, PASS], F32, name="y", bufs=4)
-                words = stage.tile([P, PASS], BF16, name="y_bf16", bufs=6)
-                y_words[c, h] = words
+            y_needs(c, h)
+
+            def run(number):
+                bank = last_stage(c, h, 0, PASS)
+                total, y = y_tiles(c, h)
 
                 def add():
-                    nc.vector.tensor_tensor(out=total[:], in0=bank[:], in1=small["views"][:, c, cols], op=ALU.add)
+                    nc.vector.tensor_tensor(out=total[:], in0=bank[:], in1=views_sb[:, c, h * PASS:(h + 1) * PASS], op=ALU.add)
 
                 def scale():
                     ensure(("add", c, h))
-                    nc.vector.tensor_tensor(out=y[:], in0=total[:], in1=small["aversion"][:, cols], op=ALU.mult)
-                    nc.sync.dma_start(out=out_0[c * P:(c + 1) * P, cols], in_=y[:])
+                    scale_and_store(c, h, total, y)
 
-                def round_words():
+                def round_pairs():
                     ensure(("scale", c, h))
-                    nc.scalar.copy(
-                        out=words[:].rearrange("p (u m e) -> p u m e", u=2, e=2),
-                        in_=y[:].rearrange("p (m u e) -> p u m e", u=2, e=2),
-                    )
-                after(tick, Y_ADD, add, ("add", c, h))
-                after(tick, Y_MUL, scale, ("scale", c, h))
-                after(tick, Y_CAST, round_words, ("words", c, h))
+                    nc.scalar.copy(out=y_pairs[c, h][:].rearrange("p (u m e) -> p u m e", u=2, e=2), in_=by_pairs(y[:]))
+
+                after(number, 1, ("add", c, h), add)
+                after(number, 2, ("scale", c, h), scale)
+                after(number, LAG, ("pairs", c, h), round_pairs)
+
             jobs.append(run)
 
         def last_y_jobs(c, h):
-            cols = slice(h * PASS, (h + 1) * PASS)
-            tiles = {}
+            width = PASS // 2
+            for i in range(2):
+                y_needs(c, h)
 
-            def piece(i):
-                half = slice(i * 2 * P, (i + 1) * 2 * P)
-                needs[len(jobs)].extend([("positions", g, c) for g in range(3)])
-
-                def run(tick):
-                    bank = bank_tile()
-                    for g in range(GROUPS):
-                        matmul(bank[:, : 2 * P], window(positions[g, c], 0, P), window(drag[g, h], i, 2 * P), g == 0, g == GROUPS - 1)
+                def run(number, i=i):
+                    bank = last_stage(c, h, i, width)
                     if i == 0:
-                        tiles["total"] = stage.tile([P, PASS], F32, name="total", bufs=3)
-                        tiles["y"] = stage.tile([P, PASS], F32, name="y", bufs=4)
-                        y_words[c, h] = stage.tile([P, PASS], BF16, name="y_bf16", bufs=6)
-                    total = tiles["total"]
+                        shared["y"] = y_tiles(c, h)
+                    total, y = shared["y"]
+                    piece = slice(i * width, (i + 1) * width)
+                    cols = slice(h * PASS + piece.start, h * PASS + piece.stop)
 
                     def add():
-                        nc.vector.tensor_tensor(out=total[:, half], in0=bank[:, : 2 * P], in1=small["views"][:, c, cols][:, half], op=ALU.add)
+                        nc.vector.tensor_tensor(out=total[:, piece], in0=bank[:, :width], in1=views_sb[:, c, cols], op=ALU.add)
 
-                    def words():
-                        ensure(("add", c, h, i))
-                        nc.vector.tensor_tensor(
-                            out=y_words[c, h][:].rearrange("p (u m e) -> p u m e", u=2, e=2)[:, :, i * 64:(i + 1) * 64, :],
-                            in0=total[:, half].rearrange("p (m u e) -> p u m e", u=2, e=2),
-                            in1=small["aversion"][:, cols][:, half].rearrange("p (m u e) -> p u m e", u=2, e=2), op=ALU.mult)
-
-                    def both():
+                    def round_pairs():
                         ensure(("add", c, h, 1))
-                        ensure(("piece", c, h, 0))
-                        words()
+                        ensure(("pairs", c, h, 0))
+                        rounded = y_pairs[c, h][:].rearrange("p (u m e) -> p u m e", u=2, e=2)
+                        nc.vector.tensor_tensor(out=rounded[:, :, i * P // 2:(i + 1) * P // 2, :], in0=by_pairs(total[:, piece]),
+                                                in1=by_pairs(aversion_sb[:, cols]), op=ALU.mult)
 
-                    def scale():
-                        nc.vector.tensor_tensor(out=tiles["y"][:], in0=total[:], in1=small["aversion"][:, cols], op=ALU.mult)
-                        nc.sync.dma_start(out=out_0[c * P:(c + 1) * P, cols], in_=tiles["y"][:])
-                    after(tick, 1, add, ("add", c, h, i))
+                    after(number, 1, ("add", c, h, i), add)
                     if i == 0:
-                        after(tick, 3, words, ("piece", c, h, 0))
+                        after(number, 3, ("pairs", c, h, 0), round_pairs)
                     else:
-                        after(tick, 2, both, ("words", c, h))
-                        after(tick, 3, scale)
+                        after(number, 2, ("pairs", c, h), round_pairs)
+                        after(number, 3, ("scale", c, h), lambda: scale_and_store(c, h, total, y))
+
                 jobs.append(run)
-            piece(0)
-            piece(1)
 
         def planes_job(c, h):
-            needs[len(jobs)].append(("words", c, h))
-            def run(tick):
+            needs[len(jobs)].append(("pairs", c, h))
+
+            def run(number):
                 bank = bank_tile()
                 for u in range(2):
-                    nc.tensor.transpose(bank[:, u * P:(u + 1) * P], y_words[c, h][:].bitcast(F32)[:, u * P:(u + 1) * P], ident[:])
+                    nc.tensor.transpose(bank[:, u * P:(u + 1) * P], y_pairs[c, h][:].bitcast(F32)[:, u * P:(u + 1) * P], ident[:])
                 turned = stage.tile([P, PASS], BF16, name="y_turned", align_bytes=64)
                 nc.scalar.copy(
                     out=turned[:].bitcast(F32).rearrange("p (m u) -> p m u", u=2),
                     in_=bank[:, : 2 * P].rearrange("p (u m) -> p m u", u=2),
                 )
-                books = slice(c * P, (c + 1) * P)
 
                 def finish():
+                    books = slice(c * P, (c + 1) * P)
                     quantize((y_codes[h][:, books], y_scales[:, h, books]), turned[:])
-                    nc.sync.dma_start(
-                        out=out_1[h].rearrange("p m t -> p (m t)").bitcast(I32)[:, books],
-                        in_=y_codes[h][:, books].bitcast(I32),
-                    )
-                after(tick, 1, finish)
+                    if c % 2 == 1:
+                        stored = slice((c - 1) * P, (c + 1) * P)
+                        nc.sync.dma_start(
+                            out=out_1[h].rearrange("p m t -> p (m t)").bitcast(I32)[:, stored],
+                            in_=y_codes[h][:, stored].bitcast(I32),
+                        )
+
+                after(number, 3, ("planes", c, h), finish)
+
             jobs.append(run)
 
-        def weave(name, g, run_length, matmul_jobs):
-            units = 2 * passes[name]
-            runs = units // run_length
-            share = len(matmul_jobs) // runs
-            for r in range(runs):
-                for unit in range(r * run_length, (r + 1) * run_length):
-                    transpose_job(name, g, unit)
-                for job, args in matmul_jobs[r * share:(r + 1) * share]:
-                    job(*args)
-
-        def drag_jobs(g, h):
-            return [(drag_job, (g, h, c)) for c in range(PACK)]
-
-        def positions_jobs(g):
-            return [(positions_job, (g, c)) for c in range(CHUNKS)]
-
         warm_bf16 = keep.tile([P, PASS], BF16, name="warm_bf16", align_bytes=64)
-        warm = window(mx_tiles("warm", P), 0, P)
+        warm = mx_tiles("warm", P)
         nc.vector.memset(warm_bf16[:], 0.0)
         quantize(warm, warm_bf16[:])
 
         def warm_job(count):
-            def run(tick):
+            def run(number):
                 bank = bank_tile()
                 for i in range(count):
                     matmul(bank[:, :P], warm, warm, True, True)
-            if count:
-                jobs.append(run)
 
-        keys = [("directions", j, a) for j in range(3) for a in range(3)] + [("alpha", 0, a) for a in range(4)]
-        for key, tick in zip(keys, FILL):
-            interleave(key, tick, "vector")
-        for word in END.split():
-            kind, i, j = word[0], int(word[1]), int(word[2])
-            if kind == "W":
-                warm_job(10 * i + j)
-            elif kind == "R":
-                transpose_job("risk", i, j)
-            elif kind == "S":
-                transpose_job("signals", i, j)
-            elif kind == "D":
-                drag_job(i, j // 4, j % 4)
-            else:
-                {"P": positions_job, "Y": y_job, "T": planes_job, "Z": last_y_jobs}[kind](i, j)
+            jobs.append(run)
 
-        for tick in range(len(jobs) + 8):
-            for lag, task in sorted(later[tick], key=lambda entry: entry[0]):
-                task()
-            for ahead in range(LOOK + 1):
-                for key in needs[tick + ahead]:
-                    ensure(key)
-            if tick < len(jobs):
-                jobs[tick](tick)
+        def transposes(name, g, units):
+            for unit in units:
+                transpose_job(name, g, unit)
+
+        for a, key in enumerate(passes_of("directions", 0)):
+            interleave(key)
+            warm_job(WARM_BETWEEN if a else WARM_FIRST)
+            transposes("risk", 0, (2 * a, 2 * a + 1))
+        second_strip = passes_of("directions", 1)
+        transposes("risk", 1, range(2))
+        drag_job(0, 0)
+        interleave(second_strip[0])
+        drag_job(0, 1)
+        interleave(second_strip[1])
+        transposes("risk", 1, range(2, 6))
+        drag_job(1, 0)
+        interleave(second_strip[2])
+        drag_job(1, 1)
+        halves = [("risk", 2, range(3 * i, 3 * i + 3)) for i in range(2)]
+        halves.extend(("signals", g, range(4 * i, 4 * i + 4)) for g in range(GROUPS) for i in range(2))
+        drag_rounds = [[(g, chunk) for chunk in (2, 3)] for g in range(2)]
+        drag_rounds.append([(2, chunk) for chunk in range(PACK)])
+        drag_rounds.extend([(g, chunk) for chunk in range(PACK, 2 * PACK)] for g in range(GROUPS))
+        to_interleave = passes_of("directions", 2) + passes_of("alpha", 0)
+        for r, work in enumerate(drag_rounds):
+            transposes(*halves[r])
+            for i, (g, chunk) in enumerate(work):
+                if i == 0 or (i == 2 and r == len(drag_rounds) - 1):
+                    interleave(to_interleave[r + i // 2])
+                drag_job(g, chunk)
+        for g, half in enumerate(halves[len(drag_rounds):]):
+            transposes(*half)
+            positions_jobs(g, 0, 2)
+        positions_jobs(GROUPS - 1, 0, 2)
+        singles = [(g, chunk) for chunk in (2, 3) for g in range(GROUPS)]
+        tiles = [(c, h) for c in range(BOOK_CHUNKS) for h in range(HALVES)]
+        positions_jobs(*singles[0], 1)
+        for single, tile in zip(singles[1:], tiles):
+            positions_jobs(*single, 1)
+            y_job(*tile)
+        for tile in tiles[:4]:
+            planes_job(*tile)
+        for tile in tiles[len(singles) - 1: -1]:
+            y_job(*tile)
+        last_y_jobs(*tiles[-1])
+        for tile in tiles[4:]:
+            planes_job(*tile)
+
+        for number in range(len(jobs) + LAG):
+            for distance, name in sorted(due[number], key=lambda entry: entry[0]):
+                ensure(name)
+            for ahead in range(LAG + 1):
+                for name in needs[number + ahead]:
+                    ensure(name)
+            if number < len(jobs):
+                jobs[number](number)
 
         scale_rows = out_2.bitcast(I32).rearrange("h q m -> q h m")
         for quadrant in range(4):

@@ -23,12 +23,14 @@ GROUPS = A // PASS
 BOOK_CHUNKS = B // P
 HALVES = D // PASS
 PASSES = {"risk": A // PASS, "signals": K // PASS}
+UNITS = {"risk": PACK * (A // PASS) // 2, "signals": PACK * (K // PASS) // 2}
 STRIPS = {"directions": [(0, 2), (2, 2), (4, 4)], "alpha": [(0, 4)]}
 
 LAG = 4
+SORT_LEAD = 5
 UNSORTED_GROUPS = 2
-WARM_FIRST, WARM_BETWEEN = 30, 6
 RAW_BUFS = 9
+Y_PAIRS_BUFS = 6
 TURNED_BUFS = 16
 
 
@@ -148,8 +150,8 @@ def tile_book_risk_drag_h3_kernel(
                 release(key)
                 mx = mx_tiles("%s_%d_%d" % key, count * P)
                 for chunks in (1, 2):
-                    for c in range(0, count, chunks):
-                        moving[name, first + c, chunks, a] = window(mx, c // chunks, chunks * P)
+                    for i in range(count // chunks):
+                        moving[name, first + i * chunks, chunks, a] = window(mx, i, chunks * P)
                 after(number, 1, key, lambda: quantize(mx, grouped[:].rearrange("p n t -> p (n t)")))
 
             after(number, 0, ("interleave",) + key, copy)
@@ -169,17 +171,17 @@ def tile_book_risk_drag_h3_kernel(
             sorted_pairs[key] = tile
 
         def transpose_job(name, g, unit):
-            parts = [divmod(n, PASSES[name]) for n in (2 * unit, 2 * unit + 1)]
+            slot_passes = [divmod(n, PASSES[name]) for n in (2 * unit, 2 * unit + 1)]
             is_sorted = name == "signals" or g >= UNSORTED_GROUPS
             merged = 2 if is_sorted else 1
-            lead = LAG if name == "signals" else 1
-            for t, a in parts:
+            lead = SORT_LEAD if name == "signals" else 1
+            for t, a in slot_passes:
                 if is_sorted and a == 0:
                     after(len(jobs) - lead, 0, ("sort", name, g, t), lambda t=t: sort_pairs((name, g, t)))
 
             def run(number):
                 bank = bank_tile()
-                for i, (t, a) in enumerate(parts):
+                for i, (t, a) in enumerate(slot_passes):
                     for u in range(2):
                         if is_sorted:
                             src = sorted_pairs[name, g, t][:, u, a, :]
@@ -198,7 +200,7 @@ def tile_book_risk_drag_h3_kernel(
                     out=turned[:, part * 2 * PASS:(part + 1) * 2 * PASS].bitcast(F32).rearrange("p (i m u) -> p i m u", i=2, u=2),
                     in_=bank[:].rearrange("p (i u m) -> p i m u", i=2, u=2),
                 )
-                for i, (t, a) in enumerate(parts):
+                for i, (t, a) in enumerate(slot_passes):
                     stationary[name, g, t, a] = window(mx, 2 * (unit % 2) + i, P)
                 if part == merged - 1:
                     after(number, LAG, (name, g, unit),
@@ -216,13 +218,13 @@ def tile_book_risk_drag_h3_kernel(
         drag = {(g, h): mx_tiles("drag_%d_%d" % (g, h), PASS) for g in range(GROUPS) for h in range(HALVES)}
 
         def drag_job(g, chunk):
-            h, c = divmod(chunk, PACK)
-            needs[len(jobs)].extend([("risk", g, unit) for unit in range(2 * PASSES["risk"])] + strip_passes("directions", chunk))
+            h, inside = divmod(chunk, PACK)
+            needs[len(jobs)].extend([("risk", g, unit) for unit in range(UNITS["risk"])] + strip_passes("directions", chunk))
 
             def run(number):
                 bank = bank_tile()
                 first_stage(bank, "risk", "directions", g, range(PACK), chunk, 1)
-                part = c % 2
+                part = chunk % 2
                 if part == 0:
                     shared["drag"] = stage.tile([P, 2 * P, PACK], BF16, name="drag_bf16", align_bytes=64)
                 rounded = shared["drag"]
@@ -230,7 +232,7 @@ def tile_book_risk_drag_h3_kernel(
                                      func=ACT.Copy, scale=-1.0)
                 if part == 1:
                     after(number, LAG, ("drag", g, chunk),
-                          lambda: quantize(window(drag[g, h], c // 2, 2 * P), rounded[:].rearrange("p n t -> p (n t)")))
+                          lambda: quantize(window(drag[g, h], inside // 2, 2 * P), rounded[:].rearrange("p n t -> p (n t)")))
 
             jobs.append(run)
 
@@ -240,8 +242,8 @@ def tile_book_risk_drag_h3_kernel(
         def positions_jobs(g, chunk, chunks):
             per_bank = PACK // chunks
             width = chunks * P
-            for c in range(chunks):
-                made_by[g, chunk + c] = ("positions", g, chunk)
+            for i in range(chunks):
+                made_by[g, chunk + i] = ("positions", g, chunk)
             for v in range(chunks):
                 units = range(2 * per_bank * v, 2 * per_bank * (v + 1))
                 needs[len(jobs)].extend([("signals", g, unit) for unit in units] + passes_of("alpha", 0))
@@ -252,19 +254,19 @@ def tile_book_risk_drag_h3_kernel(
                     if v == 0:
                         shared["squashed"] = stage.tile([P, chunks, width, per_bank], F32, name="squashed")
                     squashed = shared["squashed"]
-                    nc.scalar.activation(out=squashed[:, v], in_=bank[:].rearrange("p (u n) -> p n u", u=per_bank), func=ACT.Tanh)
+                    nc.scalar.activation(out=squashed[:, v], in_=bank[:].rearrange("p (j n) -> p n j", j=per_bank), func=ACT.Tanh)
                     if v < chunks - 1:
                         return
                     rounded = stage.tile([P, width, PACK], BF16, name="positions_bf16", align_bytes=64)
                     mx = mx_tiles("positions_%d_%d" % (g, chunk), width)
-                    for c in range(chunks):
-                        positions[g, chunk + c] = window(mx, c, P)
+                    for i in range(chunks):
+                        positions[g, chunk + i] = window(mx, i, P)
 
                     def times_limit():
-                        factor = limit_sb[:, g, :].rearrange("p (v u) -> p v u", v=chunks).unsqueeze(1)
+                        factor = limit_sb[:, g, :].rearrange("p (v j) -> p v j", v=chunks).unsqueeze(1)
                         nc.vector.tensor_tensor(
-                            out=rounded[:].rearrange("p n (v u) -> p n v u", v=chunks),
-                            in0=squashed[:].rearrange("p v n u -> p n v u"),
+                            out=rounded[:].rearrange("p n (v j) -> p n v j", v=chunks),
+                            in0=squashed[:].rearrange("p v n j -> p n v j"),
                             in1=factor.to_broadcast([P, width, chunks, per_bank]), op=ALU.mult,
                         )
 
@@ -299,7 +301,7 @@ def tile_book_risk_drag_h3_kernel(
         def y_tiles(c, h):
             total = stage.tile([P, PASS], F32, name="total")
             y = stage.tile([P, PASS], F32, name="y", bufs=LAG)
-            y_pairs[c, h] = stage.tile([P, PASS], BF16, name="y_bf16", bufs=6)
+            y_pairs[c, h] = stage.tile([P, PASS], BF16, name="y_bf16", bufs=Y_PAIRS_BUFS)
             return total, y
 
         def scale_and_store(c, h, total, y):
@@ -386,20 +388,7 @@ def tile_book_risk_drag_h3_kernel(
                             in_=y_codes[h][:, stored].bitcast(I32),
                         )
 
-                after(number, 3, ("planes", c, h), finish)
-
-            jobs.append(run)
-
-        warm_bf16 = keep.tile([P, PASS], BF16, name="warm_bf16", align_bytes=64)
-        warm = mx_tiles("warm", P)
-        nc.vector.memset(warm_bf16[:], 0.0)
-        quantize(warm, warm_bf16[:])
-
-        def warm_job(count):
-            def run(number):
-                bank = bank_tile()
-                for i in range(count):
-                    matmul(bank[:, :P], warm, warm, True, True)
+                after(number, LAG - 1, ("planes", c, h), finish)
 
             jobs.append(run)
 
@@ -409,7 +398,6 @@ def tile_book_risk_drag_h3_kernel(
 
         for a, key in enumerate(passes_of("directions", 0)):
             interleave(key)
-            warm_job(WARM_BETWEEN if a else WARM_FIRST)
             transposes("risk", 0, (2 * a, 2 * a + 1))
         second_strip = passes_of("directions", 1)
         transposes("risk", 1, range(2))
@@ -417,38 +405,40 @@ def tile_book_risk_drag_h3_kernel(
         interleave(second_strip[0])
         drag_job(0, 1)
         interleave(second_strip[1])
-        transposes("risk", 1, range(2, 6))
+        transposes("risk", 1, range(2, UNITS["risk"]))
         drag_job(1, 0)
         interleave(second_strip[2])
         drag_job(1, 1)
-        halves = [("risk", 2, range(3 * i, 3 * i + 3)) for i in range(2)]
-        halves.extend(("signals", g, range(4 * i, 4 * i + 4)) for g in range(GROUPS) for i in range(2))
-        drag_rounds = [[(g, chunk) for chunk in (2, 3)] for g in range(2)]
-        drag_rounds.append([(2, chunk) for chunk in range(PACK)])
+        last = GROUPS - 1
+        to_turn = [("risk", last)] + [("signals", g) for g in range(GROUPS)]
+        half_groups = [(name, g, range(i * UNITS[name] // 2, (i + 1) * UNITS[name] // 2)) for name, g in to_turn for i in range(2)]
+        drag_rounds = [[(g, chunk) for chunk in (2, 3)] for g in range(last)]
+        drag_rounds.append([(last, chunk) for chunk in range(PACK)])
         drag_rounds.extend([(g, chunk) for chunk in range(PACK, 2 * PACK)] for g in range(GROUPS))
         to_interleave = passes_of("directions", 2) + passes_of("alpha", 0)
         for r, work in enumerate(drag_rounds):
-            transposes(*halves[r])
+            transposes(*half_groups[r])
             for i, (g, chunk) in enumerate(work):
                 if i == 0 or (i == 2 and r == len(drag_rounds) - 1):
                     interleave(to_interleave[r + i // 2])
                 drag_job(g, chunk)
-        for g, half in enumerate(halves[len(drag_rounds):]):
-            transposes(*half)
+        for g, half_group in enumerate(half_groups[len(drag_rounds):]):
+            transposes(*half_group)
             positions_jobs(g, 0, 2)
-        positions_jobs(GROUPS - 1, 0, 2)
+        positions_jobs(last, 0, 2)
         singles = [(g, chunk) for chunk in (2, 3) for g in range(GROUPS)]
         tiles = [(c, h) for c in range(BOOK_CHUNKS) for h in range(HALVES)]
         positions_jobs(*singles[0], 1)
         for single, tile in zip(singles[1:], tiles):
             positions_jobs(*single, 1)
             y_job(*tile)
-        for tile in tiles[:4]:
+        early = 2 * HALVES
+        for tile in tiles[:early]:
             planes_job(*tile)
         for tile in tiles[len(singles) - 1: -1]:
             y_job(*tile)
         last_y_jobs(*tiles[-1])
-        for tile in tiles[4:]:
+        for tile in tiles[early:]:
             planes_job(*tile)
 
         for number in range(len(jobs) + LAG):

from collections import defaultdict
from contextlib import ExitStack

import concourse.mybir as mybir
from concourse.masks import make_identity

A, K, B, D = 1536, 2048, 512, 1024
FLOPS = 2 * A * K * B + 2 * A * A * D + 2 * A * B * D

F32 = mybir.dt.float32
BF16 = mybir.dt.bfloat16
U32 = mybir.dt.uint32
I32 = mybir.dt.int32
U8 = mybir.dt.uint8
FP8X4 = mybir.dt.float8_e4m3fn_x4
ACT = mybir.ActivationFunctionType
ALU = mybir.AluOpType

P = 128
PACK = 4
PASS = P * PACK
GROUPS = A // PASS
BOOK_CHUNKS = B // P
HALVES = D // PASS
PASSES = {"risk": A // PASS, "signals": K // PASS}
UNITS = {"risk": PACK * (A // PASS) // 2, "signals": PACK * (K // PASS) // 2}
STRIPS = {"directions": [(0, 2), (2, 2), (4, 4)], "alpha": [(0, 4)]}

LAG = 4
SORT_LEAD = 5
UNSORTED_GROUPS = 2
RAW_BUFS = 9
Y_PAIRS_BUFS = 6
TURNED_BUFS = 16


def tile_book_risk_drag_h3_kernel(
    tc, signals, alpha, limit, risk, directions, views, aversion, out_0, out_1, out_2
):
    nc = tc.nc
    with ExitStack() as ctx:
        keep = ctx.enter_context(tc.tile_pool(name="keep", bufs=1))
        raw_pool = ctx.enter_context(tc.tile_pool(name="raw", bufs=RAW_BUFS))
        stage = ctx.enter_context(tc.tile_pool(name="stage", bufs=3))
        psum = ctx.enter_context(tc.psum_pool(name="psum", bufs=8))
        ctx.enter_context(tc.manual_schedule())

        ident = keep.tile([P, P], F32, name="ident")
        make_identity(nc, ident[:])

        def mx_tiles(name, width, pool=keep, bufs=None):
            codes = pool.tile([P, width], U32, name=name + "_codes", bufs=bufs, align_bytes=64)
            scales = pool.tile([P, width], U8, name=name + "_scales", bufs=bufs, align_bytes=64)
            return codes[:], scales[:]

        def window(mx, i, width):
            cols = slice(i * width, (i + 1) * width)
            return mx[0][:, cols], mx[1][:, cols]

        def quantize(mx, src):
            nc.vector.quantize_mx(out=mx[0].bitcast(FP8X4), scales=mx[1], in_=src)

        def matmul(out, stationary, moving, start, stop):
            nc.tensor.matmul_mx(
                out=out, lhsT=stationary[0].bitcast(FP8X4), lhsT_scale=stationary[1],
                rhs=moving[0].bitcast(FP8X4), rhs_scale=moving[1], start=start, stop=stop,
            )

        def bank_tile():
            return psum.tile([P, PASS], F32, name="bank")

        def slots_of(name, g):
            return [(name, g, t) for t in range(PACK)]

        def passes_of(name, s):
            partner = "risk" if name == "directions" else "signals"
            return [(name, s, a) for a in range(PASSES[partner])]

        def alternate(first, second):
            mixed = [key for both in zip(first, second) for key in both]
            return mixed + first[len(second):] + second[len(first):]

        order = (
            alternate(slots_of("risk", 0), passes_of("directions", 0))
            + slots_of("risk", 1) + passes_of("directions", 1) + slots_of("risk", 2)
            + alternate(passes_of("directions", 2), slots_of("signals", 0))
            + alternate(passes_of("alpha", 0), slots_of("signals", 1))
            + slots_of("signals", 2)
        )
        inputs = {"risk": risk, "signals": signals, "directions": directions, "alpha": alpha}
        raw = {}
        consumed = set()
        limit_sb = keep.tile([P, GROUPS, PACK], BF16, name="limit_sb")
        views_sb = keep.tile([P, BOOK_CHUNKS, D], BF16, name="views_sb")
        aversion_sb = keep.tile([P, D], BF16, name="aversion_sb")

        def load(key):
            name, i, j = key
            if name in PASSES:
                src = inputs[name][i * PASS:(i + 1) * PASS, :].rearrange("(m t) k -> m t k", t=PACK)[:, j, :]
                raw[key] = raw_pool.tile([P, PASSES[name] * PASS], BF16, name="raw")
            else:
                first, count = STRIPS[name][i]
                rows = inputs[name][j * PASS:(j + 1) * PASS, first * P:(first + count) * P]
                src = rows.rearrange("(p t) n -> p t n", t=PACK)
                raw[key] = raw_pool.tile([P, PACK, count * P], BF16, name="raw")
            nc.sync.dma_start(out=raw[key][:], in_=src)
            if key == ("alpha", 0, 0):
                nc.sync.dma_start(out=limit_sb[:], in_=limit.rearrange("(g p t) -> p g t", p=P, t=PACK))
            if key == order[-1]:
                nc.sync.dma_start(out=views_sb[:], in_=views.rearrange("(c p) d -> p c d", p=P))
                nc.sync.dma_start(out=aversion_sb[:], in_=aversion.partition_broadcast(P))

        def issue_loads():
            while len(raw) < len(order) and all(key in consumed for key in order[: max(0, len(raw) - RAW_BUFS + 1)]):
                load(order[len(raw)])

        def release(key):
            consumed.add(key)
            issue_loads()

        issue_loads()

        jobs = []
        needs = defaultdict(list)
        due = defaultdict(list)
        pending = {}

        def after(number, distance, name, step):
            pending[name] = step
            due[number + distance].append((distance, name))

        def ensure(name):
            if name in pending:
                pending.pop(name)()

        moving = {}

        def interleave(key):
            name, s, a = key
            first, count = STRIPS[name][s]
            number = len(jobs)

            def copy():
                grouped = stage.tile([P, count * P, PACK], BF16, name="grouped", bufs=2, align_bytes=64)
                nc.vector.tensor_copy(
                    out=grouped[:].rearrange("p (c i) t -> p c t i", i=4),
                    in_=raw[key][:].rearrange("p t (c i) -> p c t i", i=4),
                )
                release(key)
                mx = mx_tiles("%s_%d_%d" % key, count * P)
                for chunks in (1, 2):
                    for i in range(count // chunks):
                        moving[name, first + i * chunks, chunks, a] = window(mx, i, chunks * P)
                after(number, 1, key, lambda: quantize(mx, grouped[:].rearrange("p n t -> p (n t)")))

            after(number, 0, ("interleave",) + key, copy)

        def strip_passes(name, chunk):
            s = [first <= chunk < first + count for first, count in STRIPS[name]].index(True)
            return passes_of(name, s)

        sorted_pairs = {}
        stationary = {}
        shared = {}

        def sort_pairs(key):
            tile = stage.tile([P, 2, PASSES[key[0]], P], F32, name="sorted", bufs=PACK)
            nc.vector.tensor_copy(out=tile[:], in_=raw[key][:].bitcast(F32).rearrange("p (a m u) -> p u a m", m=P, u=2))
            release(key)
            sorted_pairs[key] = tile

        def transpose_job(name, g, unit):
            slot_passes = [divmod(n, PASSES[name]) for n in (2 * unit, 2 * unit + 1)]
            is_sorted = name == "signals" or g >= UNSORTED_GROUPS
            merged = 2 if is_sorted else 1
            lead = SORT_LEAD if name == "signals" else 1
            for t, a in slot_passes:
                if is_sorted and a == 0:
                    after(len(jobs) - lead, 0, ("sort", name, g, t), lambda t=t: sort_pairs((name, g, t)))

            def run(number):
                bank = bank_tile()
                for i, (t, a) in enumerate(slot_passes):
                    for u in range(2):
                        if is_sorted:
                            src = sorted_pairs[name, g, t][:, u, a, :]
                        else:
                            src = raw[name, g, t][:].bitcast(F32)[:, 2 * P * a + u: 2 * P * (a + 1): 2]
                        nc.tensor.transpose(bank[:, (2 * i + u) * P:(2 * i + u + 1) * P], src, ident[:])
                    if not is_sorted and a == PASSES[name] - 1:
                        release((name, g, t))
                part = unit % merged
                if part == 0:
                    shared["turned"] = stage.tile([P, merged * 2 * PASS], BF16, name="turned", bufs=LAG, align_bytes=64)
                if unit % 2 == 0:
                    shared["turned_mx"] = mx_tiles("turned", 4 * P, pool=stage, bufs=TURNED_BUFS)
                turned, mx = shared["turned"], shared["turned_mx"]
                nc.scalar.copy(
                    out=turned[:, part * 2 * PASS:(part + 1) * 2 * PASS].bitcast(F32).rearrange("p (i m u) -> p i m u", i=2, u=2),
                    in_=bank[:].rearrange("p (i u m) -> p i m u", i=2, u=2),
                )
                for i, (t, a) in enumerate(slot_passes):
                    stationary[name, g, t, a] = window(mx, 2 * (unit % 2) + i, P)
                if part == merged - 1:
                    after(number, LAG, (name, g, unit),
                          lambda: quantize(window(mx, (unit % 2) // merged, merged * 2 * P), turned[:]))

            jobs.append(run)

        def first_stage(bank, name, partner, g, slots, chunk, chunks):
            width = chunks * P
            for i, t in enumerate(slots):
                for a in range(PASSES[name]):
                    matmul(bank[:, i * width:(i + 1) * width], stationary[name, g, t, a], moving[partner, chunk, chunks, a],
                           a == 0, a == PASSES[name] - 1)

        drag = {(g, h): mx_tiles("drag_%d_%d" % (g, h), PASS) for g in range(GROUPS) for h in range(HALVES)}

        def drag_job(g, chunk):
            h, inside = divmod(chunk, PACK)
            needs[len(jobs)].extend([("risk", g, unit) for unit in range(UNITS["risk"])] + strip_passes("directions", chunk))

            def run(number):
                bank = bank_tile()
                first_stage(bank, "risk", "directions", g, range(PACK), chunk, 1)
                part = chunk % 2
                if part == 0:
                    shared["drag"] = stage.tile([P, 2 * P, PACK], BF16, name="drag_bf16", align_bytes=64)
                rounded = shared["drag"]
                nc.scalar.activation(out=rounded[:, part * P:(part + 1) * P, :], in_=bank[:].rearrange("p (t n) -> p n t", t=PACK),
                                     func=ACT.Copy, scale=-1.0)
                if part == 1:
                    after(number, LAG, ("drag", g, chunk),
                          lambda: quantize(window(drag[g, h], inside // 2, 2 * P), rounded[:].rearrange("p n t -> p (n t)")))

            jobs.append(run)

        positions = {}
        made_by = {}

        def positions_jobs(g, chunk, chunks):
            per_bank = PACK // chunks
            width = chunks * P
            for i in range(chunks):
                made_by[g, chunk + i] = ("positions", g, chunk)
            for v in range(chunks):
                units = range(2 * per_bank * v, 2 * per_bank * (v + 1))
                needs[len(jobs)].extend([("signals", g, unit) for unit in units] + passes_of("alpha", 0))

                def run(number, v=v):
                    bank = bank_tile()
                    first_stage(bank, "signals", "alpha", g, range(per_bank * v, per_bank * (v + 1)), chunk, chunks)
                    if v == 0:
                        shared["squashed"] = stage.tile([P, chunks, width, per_bank], F32, name="squashed")
                    squashed = shared["squashed"]
                    nc.scalar.activation(out=squashed[:, v], in_=bank[:].rearrange("p (j n) -> p n j", j=per_bank), func=ACT.Tanh)
                    if v < chunks - 1:
                        return
                    rounded = stage.tile([P, width, PACK], BF16, name="positions_bf16", align_bytes=64)
                    mx = mx_tiles("positions_%d_%d" % (g, chunk), width)
                    for i in range(chunks):
                        positions[g, chunk + i] = window(mx, i, P)

                    def times_limit():
                        factor = limit_sb[:, g, :].rearrange("p (v j) -> p v j", v=chunks).unsqueeze(1)
                        nc.vector.tensor_tensor(
                            out=rounded[:].rearrange("p n (v j) -> p n v j", v=chunks),
                            in0=squashed[:].rearrange("p v n j -> p n v j"),
                            in1=factor.to_broadcast([P, width, chunks, per_bank]), op=ALU.mult,
                        )

                    def finish():
                        ensure(("limit", g, chunk))
                        quantize(mx, rounded[:].rearrange("p n t -> p (n t)"))

                    after(number, 2, ("limit", g, chunk), times_limit)
                    after(number, 3, ("positions", g, chunk), finish)

                jobs.append(run)

        y_pairs = {}
        y_codes = [keep.tile([P, B], U32, name="y_codes_%d" % h, align_bytes=64) for h in range(HALVES)]
        y_scales = keep.tile([P, HALVES, B], U8, name="y_scales", align_bytes=64)

        def by_pairs(ap):
            return ap.rearrange("p (m u e) -> p u m e", u=2, e=2)

        def last_stage(c, h, i, width):
            bank = bank_tile()
            for g in range(GROUPS):
                matmul(bank[:, :width], positions[g, c], window(drag[g, h], i, width), g == 0, g == GROUPS - 1)
            return bank

        def y_needs(c, h):
            needs[len(jobs)].extend(
                [made_by[g, c] for g in range(GROUPS)]
                + [("drag", g, PACK * h + i) for g in range(GROUPS) for i in range(PACK)]
            )

        def y_tiles(c, h):
            total = stage.tile([P, PASS], F32, name="total")
            y = stage.tile([P, PASS], F32, name="y", bufs=LAG)
            y_pairs[c, h] = stage.tile([P, PASS], BF16, name="y_bf16", bufs=Y_PAIRS_BUFS)
            return total, y

        def scale_and_store(c, h, total, y):
            cols = slice(h * PASS, (h + 1) * PASS)
            nc.vector.tensor_tensor(out=y[:], in0=total[:], in1=aversion_sb[:, cols], op=ALU.mult)
            nc.sync.dma_start(out=out_0[c * P:(c + 1) * P, cols], in_=y[:])

        def y_job(c, h):
            y_needs(c, h)

            def run(number):
                bank = last_stage(c, h, 0, PASS)
                total, y = y_tiles(c, h)

                def add():
                    nc.vector.tensor_tensor(out=total[:], in0=bank[:], in1=views_sb[:, c, h * PASS:(h + 1) * PASS], op=ALU.add)

                def scale():
                    ensure(("add", c, h))
                    scale_and_store(c, h, total, y)

                def round_pairs():
                    ensure(("scale", c, h))
                    nc.scalar.copy(out=y_pairs[c, h][:].rearrange("p (u m e) -> p u m e", u=2, e=2), in_=by_pairs(y[:]))

                after(number, 1, ("add", c, h), add)
                after(number, 2, ("scale", c, h), scale)
                after(number, LAG, ("pairs", c, h), round_pairs)

            jobs.append(run)

        def last_y_jobs(c, h):
            width = PASS // 2
            for i in range(2):
                y_needs(c, h)

                def run(number, i=i):
                    bank = last_stage(c, h, i, width)
                    if i == 0:
                        shared["y"] = y_tiles(c, h)
                    total, y = shared["y"]
                    piece = slice(i * width, (i + 1) * width)
                    cols = slice(h * PASS + piece.start, h * PASS + piece.stop)

                    def add():
                        nc.vector.tensor_tensor(out=total[:, piece], in0=bank[:, :width], in1=views_sb[:, c, cols], op=ALU.add)

                    def round_pairs():
                        ensure(("add", c, h, 1))
                        ensure(("pairs", c, h, 0))
                        rounded = y_pairs[c, h][:].rearrange("p (u m e) -> p u m e", u=2, e=2)
                        nc.vector.tensor_tensor(out=rounded[:, :, i * P // 2:(i + 1) * P // 2, :], in0=by_pairs(total[:, piece]),
                                                in1=by_pairs(aversion_sb[:, cols]), op=ALU.mult)

                    after(number, 1, ("add", c, h, i), add)
                    if i == 0:
                        after(number, 3, ("pairs", c, h, 0), round_pairs)
                    else:
                        after(number, 2, ("pairs", c, h), round_pairs)
                        after(number, 3, ("scale", c, h), lambda: scale_and_store(c, h, total, y))

                jobs.append(run)

        def planes_job(c, h):
            needs[len(jobs)].append(("pairs", c, h))

            def run(number):
                bank = bank_tile()
                for u in range(2):
                    nc.tensor.transpose(bank[:, u * P:(u + 1) * P], y_pairs[c, h][:].bitcast(F32)[:, u * P:(u + 1) * P], ident[:])
                turned = stage.tile([P, PASS], BF16, name="y_turned", align_bytes=64)
                nc.scalar.copy(
                    out=turned[:].bitcast(F32).rearrange("p (m u) -> p m u", u=2),
                    in_=bank[:, : 2 * P].rearrange("p (u m) -> p m u", u=2),
                )

                def finish():
                    books = slice(c * P, (c + 1) * P)
                    quantize((y_codes[h][:, books], y_scales[:, h, books]), turned[:])
                    if c % 2 == 1:
                        stored = slice((c - 1) * P, (c + 1) * P)
                        nc.sync.dma_start(
                            out=out_1[h].rearrange("p m t -> p (m t)").bitcast(I32)[:, stored],
                            in_=y_codes[h][:, stored].bitcast(I32),
                        )

                after(number, LAG - 1, ("planes", c, h), finish)

            jobs.append(run)

        def transposes(name, g, units):
            for unit in units:
                transpose_job(name, g, unit)

        for a, key in enumerate(passes_of("directions", 0)):
            interleave(key)
            transposes("risk", 0, (2 * a, 2 * a + 1))
        second_strip = passes_of("directions", 1)
        transposes("risk", 1, range(2))
        drag_job(0, 0)
        interleave(second_strip[0])
        drag_job(0, 1)
        interleave(second_strip[1])
        transposes("risk", 1, range(2, UNITS["risk"]))
        drag_job(1, 0)
        interleave(second_strip[2])
        drag_job(1, 1)
        last = GROUPS - 1
        to_turn = [("risk", last)] + [("signals", g) for g in range(GROUPS)]
        half_groups = [(name, g, range(i * UNITS[name] // 2, (i + 1) * UNITS[name] // 2)) for name, g in to_turn for i in range(2)]
        drag_rounds = [[(g, chunk) for chunk in (2, 3)] for g in range(last)]
        drag_rounds.append([(last, chunk) for chunk in range(PACK)])
        drag_rounds.extend([(g, chunk) for chunk in range(PACK, 2 * PACK)] for g in range(GROUPS))
        to_interleave = passes_of("directions", 2) + passes_of("alpha", 0)
        for r, work in enumerate(drag_rounds):
            transposes(*half_groups[r])
            for i, (g, chunk) in enumerate(work):
                if i == 0 or (i == 2 and r == len(drag_rounds) - 1):
                    interleave(to_interleave[r + i // 2])
                drag_job(g, chunk)
        for g, half_group in enumerate(half_groups[len(drag_rounds):]):
            transposes(*half_group)
            positions_jobs(g, 0, 2)
        positions_jobs(last, 0, 2)
        singles = [(g, chunk) for chunk in (2, 3) for g in range(GROUPS)]
        tiles = [(c, h) for c in range(BOOK_CHUNKS) for h in range(HALVES)]
        positions_jobs(*singles[0], 1)
        for single, tile in zip(singles[1:], tiles):
            positions_jobs(*single, 1)
            y_job(*tile)
        early = 2 * HALVES
        for tile in tiles[:early]:
            planes_job(*tile)
        for tile in tiles[len(singles) - 1: -1]:
            y_job(*tile)
        last_y_jobs(*tiles[-1])
        for tile in tiles[early:]:
            planes_job(*tile)

        for number in range(len(jobs) + LAG):
            for distance, name in sorted(due[number], key=lambda entry: entry[0]):
                ensure(name)
            for ahead in range(LAG + 1):
                for name in needs[number + ahead]:
                    ensure(name)
            if number < len(jobs):
                jobs[number](number)

        scale_rows = out_2.bitcast(I32).rearrange("h q m -> q h m")
        for quadrant in range(4):
            queue = nc.sync if quadrant % 2 == 0 else nc.scalar
            queue.dma_start(
                out=scale_rows[4 * quadrant: 4 * quadrant + 4],
                in_=y_scales[32 * quadrant: 32 * quadrant + 4].bitcast(I32),
            )
